import numpy as np
import ml_dtypes


def mxq(x, axis, fmt="e4m3"):
    dtype, down = {"e4m3": (ml_dtypes.float8_e4m3fn, 7), "e5m2": (ml_dtypes.float8_e5m2, 14)}[fmt]
    v = np.moveaxis(np.asarray(x, np.float32).astype(ml_dtypes.bfloat16).astype(np.float64), axis, -1)
    blocks = v.reshape(v.shape[:-1] + (-1, 32))
    amax = np.abs(blocks).max(-1, keepdims=True)
    byte = np.maximum(np.where(amax > 0, np.frexp(amax)[1] - 1 + 127, 0) - down, 1)
    scale = np.exp2(byte - 127.0)
    codes = (blocks / scale).astype(np.float32).astype(dtype).astype(np.float64)
    return np.moveaxis((codes * scale).reshape(v.shape), -1, axis)


WIDE = False


def mx_kscale(k):
    if not WIDE:
        return np.ones(k)
    levels = np.array([10, -10, 5, -5, 0])
    if k % 512:
        return np.exp2(np.random.permutation(np.resize(levels, k // 32))).repeat(32)
    a = np.empty((k // 512, 16))
    for p in range(k // 512):
        a[p, :8] = np.random.permutation(np.resize(levels, 8))
        for g in range(8):
            far = levels[np.abs(levels - a[p, g]) >= 10]
            a[p, g + 8] = far[np.random.randint(len(far))]
    return np.exp2(a.ravel()).repeat(32)


def f64(x):
    return np.asarray(x).astype(np.float64)


def striped(idx):
    return np.tile(idx.reshape(-1, 16).T, (8, 1)).astype(np.uint16)


def unstriped(offs):
    return offs[:16].T.reshape(-1).astype(np.int64)


E2M1 = np.array([0.0, 0.5, 1.0, 1.5, 2.0, 3.0, 4.0, 6.0, -0.0, -0.5, -1.0, -1.5, -2.0, -3.0, -4.0, -6.0])


def pack_weight(w, fmt):
    k, n = w.shape
    w = f64(np.asarray(w, np.float32).astype(ml_dtypes.bfloat16)).reshape(k // 32, 32, n)
    amax = np.abs(w).max(1)
    if fmt == "e4m3":
        byte = np.frexp(amax)[1] - 1 + 127 - 7
    else:
        mant, ex = np.frexp(amax / 6.0)
        byte = np.where(mant > 0.5, ex, ex - 1) + 127
    byte = np.clip(np.where(amax > 0, byte, 1), 1, 254)
    scaled = (w * np.exp2(127.0 - byte)[:, None, :]).reshape(k, n).astype(np.float32)
    by_word = np.ascontiguousarray(scaled.reshape(k // 512, 128, 4, n).transpose(0, 1, 3, 2))
    if fmt == "e4m3":
        words = by_word.astype(ml_dtypes.float8_e4m3fn).view(np.uint8)
    else:
        c = by_word.astype(ml_dtypes.float4_e2m1fn).view(np.uint8) & 0xF
        words = (c[..., 0::2] | (c[..., 1::2] << 4)).reshape(k // 512, 128, 2 * n)
    return np.ascontiguousarray(words), np.ascontiguousarray(byte.astype(np.uint8).reshape(k // 512, 16, n))


def unpack_weight(words, scales, fmt):
    g, _, n = scales.shape
    words = np.ascontiguousarray(words).reshape(g, 128, n, -1)
    if fmt == "e4m3":
        vals = words.view(ml_dtypes.float8_e4m3fn).astype(np.float64)
    else:
        nib = np.empty((g, 128, n, 4), np.uint8)
        nib[..., 0::2] = words & 0xF
        nib[..., 1::2] = words >> 4
        vals = E2M1[nib]
    vals = vals * np.repeat(np.exp2(scales.astype(np.float64) - 127.0), 8, axis=1)[..., None]
    return vals.transpose(0, 1, 3, 2).reshape(g * 512, n)


def gelu(v):
    return 0.5 * v * (1.0 + np.tanh(np.sqrt(2.0 / np.pi) * (v + 0.044715 * v**3)))


K, T, E, C, H, N = 512, 512, 4, 256, 512, 256


def by_expert(wq, xq):
    return np.concatenate([wq[e].T @ xq[:, e * C:(e + 1) * C] for e in range(E)], axis=1)


def setup_inputs():
    n = np.random.standard_normal
    s = mx_kscale(K)
    u = mx_kscale(H)
    first = np.random.permutation(np.repeat(np.arange(E), T // E))
    second = (first + 1 + np.random.permutation(np.repeat(np.arange(E - 1), -(-T // (E - 1)))[:T])) % E
    while np.bincount(second, minlength=E).max() != T // E:
        load = np.bincount(second, minlength=E); hi, lo = int(load.argmax()), int(load.argmin())
        t = np.flatnonzero((second == hi) & (first != lo))[0]; second[t] = lo
    slot_token = np.empty(E * C, np.int64); pos = np.empty((2, T), np.int64); fill = np.zeros(E, np.int64)
    place = np.stack([np.random.permutation(C) for _ in range(E)])
    for r, deal in enumerate((first, second)):
        for t in np.random.permutation(T):
            e = deal[t]; j = e * C + place[e, fill[e]]; fill[e] += 1; slot_token[j] = t; pos[r, t] = j
    g = np.random.uniform(0.2, 0.8, T)
    partner = np.concatenate([np.random.permutation(T) for _ in range(-(-E * C // T))])[:E * C]
    x = pack_weight(n((K, T)) * s[:, None], "e4m3")
    w1 = [pack_weight(m, "e2m1") for m in n((E, K, H)) / np.sqrt(K) / s[None, :, None] * u]
    wp = [pack_weight(m, "e2m1") for m in n((E, K, H)) / np.sqrt(K) / s[None, :, None] * u]
    w2 = [pack_weight(m, "e2m1") for m in n((E, H, N)) / np.sqrt(H) / u[None, :, None]]
    return {
        "x_words": x[0],
        "x_scales": x[1],
        "w1_words": np.stack([m[0] for m in w1]),
        "w1_scales": np.stack([m[1] for m in w1]),
        "wp_words": np.stack([m[0] for m in wp]),
        "wp_scales": np.stack([m[1] for m in wp]),
        "w2_words": np.stack([m[0] for m in w2]),
        "w2_scales": np.stack([m[1] for m in w2]),
        "gate": np.stack([np.tile(g, (128, 1)), np.tile(1.0 - g, (128, 1))]).astype(np.float32),
        "offs": striped(slot_token),
        "pos1": striped(pos[0]),
        "pos2": striped(pos[1]),
        "offs2": striped(partner),
    }


def reference(x_words, x_scales, w1_words, w1_scales, wp_words, wp_scales, w2_words, w2_scales, gate, offs, pos1, pos2, offs2):
    w1 = np.stack([unpack_weight(w1_words[e], w1_scales[e], "e2m1") for e in range(E)])
    wp = np.stack([unpack_weight(wp_words[e], wp_scales[e], "e2m1") for e in range(E)])
    w2 = np.stack([unpack_weight(w2_words[e], w2_scales[e], "e2m1") for e in range(E)])
    idx, idx2 = unstriped(offs), unstriped(offs2)
    x = unpack_weight(x_words, x_scales, "e4m3")
    h = gelu(by_expert(w1, x[:, idx]) + by_expert(wp, x[:, idx2]))
    y = by_expert(w2, mxq(h, 0, "e4m3"))
    out = sum(f64(gate[r, :1]) * y[:, unstriped(p)] for r, p in enumerate((pos1, pos2)))
    return out

@@ -1,0 +1,183 @@
+from contextlib import ExitStack
+
+import concourse.mybir as mybir
+from concourse.masks import make_identity
+
+K, T, E, C, H, N = 512, 512, 4, 256, 512, 256
+S = E * C
+P = 128
+FLOPS = 2 * S * (2 * K * H + H * N)
+
+F32 = mybir.dt.float32
+BF16 = mybir.dt.bfloat16
+I32 = mybir.dt.int32
+U32 = mybir.dt.uint32
+U16 = mybir.dt.uint16
+U8 = mybir.dt.uint8
+FP8X4 = mybir.dt.float8_e4m3fn_x4
+FP4X4 = mybir.dt.float4_e2m1fn_x4
+GELU = mybir.ActivationFunctionType.Gelu_apprx_tanh
+MULT = mybir.AluOpType.mult
+ADD = mybir.AluOpType.add
+
+PIECES = ((0, 256), (256, 256), (512, 256), (768, 128), (896, 128))
+
+
+def load_scale_rows(nc, plane, rows):
+    for q in range(4):
+        nc.sync.dma_start(out=plane[32 * q : 32 * q + 4].bitcast(I32), in_=rows[4 * q : 4 * q + 4])
+
+
+def tile_moe_duo_gelu_kernel(
+    tc, x_words, x_scales, w1_words, w1_scales, wp_words, wp_scales, w2_words, w2_scales, gate, offs, pos1, pos2, offs2, out
+):
+    nc = tc.nc
+    with ExitStack() as ctx:
+        keep = ctx.enter_context(tc.tile_pool(name="keep", bufs=1))
+        ring = ctx.enter_context(tc.tile_pool(name="ring", bufs=3))
+        pre_banks = ctx.enter_context(tc.psum_pool(name="pre_banks", bufs=2))
+        turn_banks = ctx.enter_context(tc.psum_pool(name="turn_banks", bufs=2))
+        y_banks = ctx.enter_context(tc.psum_pool(name="y_banks", bufs=1))
+
+        def held(name, shape, dtype):
+            return keep.tile(shape, dtype, name=name, align_bytes=64)
+
+        offs_sb = held("offs_sb", [P, S // 16], U16)
+        offs2_sb = held("offs2_sb", [P, S // 16], U16)
+        pos1_sb = held("pos1_sb", [P, T // 16], U16)
+        pos2_sb = held("pos2_sb", [P, T // 16], U16)
+        xw = held("xw", [P, T], I32)
+        xs = held("xs", [P, T], U8)
+        w1s = held("w1s", [P, E, H], U8)
+        wps = held("wps", [P, E, H], U8)
+        w2s = held("w2s", [P, E, N], U8)
+        w1w = [held("w1w%d" % a, [P, 2, 2 * H], U8) for a in range(2)]
+        wpw = [held("wpw%d" % a, [P, 2, 2 * H], U8) for a in range(2)]
+        w2w = held("w2w", [P, E, 2 * N], U8)
+        gates = held("gates", [P, 2, T], F32)
+        ident = held("ident", [P, P], F32)
+        warm_in = held("warm_in", [P, 8], F32)
+        warm_out = held("warm_out", [P, 8], F32)
+
+        def by_expert(dram):
+            return dram.bitcast(I32).rearrange("e o p n -> p (e o) n")
+
+        for plane in (xs, w1s, wps, w2s):
+            nc.vector.memset(plane[:].bitcast(I32), 0)
+        nc.vector.memset(warm_in[:], 0.0)
+        nc.scalar.activation(out=warm_out[:], in_=warm_in[:], func=GELU)
+
+        make_identity(nc, ident[:])
+
+        nc.sync.dma_start(offs_sb[:], offs)
+        nc.sync.dma_start(out=xw[:], in_=x_words.rearrange("o p t d -> p (o t d)").bitcast(I32))
+        load_scale_rows(nc, xs, x_scales.bitcast(I32).rearrange("o b t -> b (o t)"))
+        nc.sync.dma_start(offs2_sb[:], offs2)
+        nc.sync.dma_start(out=w1w[0][:].bitcast(I32), in_=by_expert(w1_words)[:, 0:2, :])
+        nc.sync.dma_start(out=wpw[0][:].bitcast(I32), in_=by_expert(wp_words)[:, 0:2, :])
+        load_scale_rows(nc, w1s, by_expert(w1_scales))
+        load_scale_rows(nc, wps, by_expert(wp_scales))
+        nc.sync.dma_start(out=w1w[1][:].bitcast(I32), in_=by_expert(w1_words)[:, 2:4, :])
+        nc.sync.dma_start(out=wpw[1][:].bitcast(I32), in_=by_expert(wp_words)[:, 2:4, :])
+        load_scale_rows(nc, w2s, by_expert(w2_scales))
+        nc.sync.dma_start(out=w2w[:].bitcast(I32), in_=by_expert(w2_words))
+        nc.sync.dma_start(pos1_sb[:], pos1)
+        nc.sync.dma_start(pos2_sb[:], pos2)
+        nc.sync.dma_start(out=gates[:], in_=gate.rearrange("r p t -> p r t"))
+
+        gathered = []
+        for first, width in PIECES:
+            cols = slice(first // 16, (first + width) // 16)
+            sides = []
+            for side, lst in enumerate((offs_sb, offs2_sb)):
+                words = held("gw%d_%d" % (first, side), [P, width], U32)
+                scales = held("gs%d_%d" % (first, side), [P, width], U8)
+                nc.vector.tensor_copy(out=words[:], in_=xw[:].bitcast(U32).indirect(lst[:, cols]))
+                nc.vector.tensor_copy(out=scales[:], in_=xs[:].indirect(lst[:, cols]))
+                sides.append((words, scales))
+            gathered.append(sides)
+
+        grouped = []
+        for (first, width), sides in zip(PIECES, gathered):
+            e = first // C
+            hq_in = held("hq_in%d" % first, [P, width, 4], BF16)
+            grouped.append(hq_in)
+            for s0 in range(0, width, P):
+                cols = slice(s0, s0 + P)
+                pre = pre_banks.tile([P, H], F32, name="pre")
+                for side, (ww, ws) in enumerate(((w1w, w1s), (wpw, wps))):
+                    words, scales = sides[side]
+                    nc.tensor.matmul_mx(
+                        out=pre[:],
+                        lhsT=words[:, cols].bitcast(FP8X4),
+                        lhsT_scale=scales[:, cols],
+                        rhs=ww[e // 2][:, e % 2, :].bitcast(FP4X4),
+                        rhs_scale=ws[:, e, :],
+                        start=(side == 0),
+                        stop=(side == 1),
+                    )
+                h = ring.tile([P, H], BF16, name="h", align_bytes=64)
+                nc.scalar.activation(
+                    out=h[:].rearrange("s (u p d) -> s u p d", u=2, d=2),
+                    in_=pre[:].rearrange("s (p u d) -> s u p d", u=2, d=2),
+                    func=GELU,
+                )
+                turned = turn_banks.tile([P, 2, P], F32, name="turned")
+                for u in range(2):
+                    nc.tensor.transpose(turned[:, u, :], h[:].bitcast(F32)[:, u * P : (u + 1) * P], ident[:])
+                nc.scalar.copy(out=hq_in[:, cols, :].bitcast(F32), in_=turned[:].rearrange("p u s -> p s u"))
+
+        ys = [held("y%d" % half, [P, S], F32) for half in range(2)]
+        runs = ((0, 1), (2, 3), (4,))
+        for r, run in enumerate(runs):
+            base = PIECES[run[0]][0]
+            total = sum(PIECES[i][1] for i in run)
+            if r < 2:
+                banks = [y_banks.tile([P, total], F32, name="yb%d_%d" % (r, half)) for half in range(2)]
+            else:
+                banks = [pre_banks.tile([P, total], F32, name="pre") for half in range(2)]
+            for i in run:
+                first, width = PIECES[i]
+                e = first // C
+                codes = held("hc%d" % first, [P, width], U32)
+                scales = held("hs%d" % first, [P, width], U8)
+                nc.vector.quantize_mx(
+                    out=codes[:].bitcast(FP8X4), scales=scales[:], in_=grouped[i][:].rearrange("p s d -> p (s d)")
+                )
+                for half in range(2):
+                    nc.tensor.matmul_mx(
+                        out=banks[half][:, first - base : first - base + width],
+                        lhsT=w2w[:, e, 2 * P * half : 2 * P * (half + 1)].bitcast(FP4X4),
+                        lhsT_scale=w2s[:, e, P * half : P * (half + 1)],
+                        rhs=codes[:].bitcast(FP8X4),
+                        rhs_scale=scales[:],
+                        start=True,
+                        stop=True,
+                    )
+            nc.vector.tensor_copy(out=ys[0][:, base : base + total], in_=banks[0][:])
+            nc.scalar.copy(out=ys[1][:, base : base + total], in_=banks[1][:])
+
+        parts = [[held("part%d_%d" % (half, r), [P, T], F32) for r in range(2)] for half in range(2)]
+        sums = [held("sum%d" % half, [P, T], F32) for half in range(2)]
+        lists = (pos1_sb, pos2_sb)
+
+        def fetch(half, r, t0, t1):
+            nc.vector.tensor_tensor(
+                parts[half][r][:, t0:t1], ys[half][:].indirect(lists[r][:, t0 // 16 : t1 // 16]), gates[:, r, t0:t1], MULT
+            )
+
+        def finish(half, t0, t1):
+            nc.vector.tensor_tensor(sums[half][:, t0:t1], parts[half][0][:, t0:t1], parts[half][1][:, t0:t1], ADD)
+            nc.sync.dma_start(out=out[P * half : P * (half + 1), t0:t1], in_=sums[half][:, t0:t1])
+
+        fetch(0, 0, 0, 512)
+        fetch(0, 1, 0, 512)
+        fetch(1, 0, 0, 256)
+        finish(0, 0, 512)
+        fetch(1, 1, 0, 256)
+        fetch(1, 0, 256, 512)
+        finish(1, 0, 256)
+        fetch(1, 1, 256, 384)
+        fetch(1, 1, 384, 512)
+        finish(1, 256, 384)
+        finish(1, 384, 512)

@@ -20,11 +20,11 @@ GELU = mybir.ActivationFunctionType.Gelu_apprx_tanh
 MULT = mybir.AluOpType.mult
 ADD = mybir.AluOpType.add
 
-PIECES = ((0, 256), (256, 256), (512, 256), (768, 128), (896, 128))
+RUNS = ((0, 512), (512, 256), (768, 128), (896, 128))
 
 
-def load_scale_rows(nc, plane, rows):
-    for q in range(4):
+def load_scale_rows(nc, plane, rows, quadrants=range(4)):
+    for q in quadrants:
         nc.sync.dma_start(out=plane[32 * q : 32 * q + 4].bitcast(I32), in_=rows[4 * q : 4 * q + 4])
 
 
@@ -62,21 +62,22 @@ def tile_moe_duo_gelu_kernel(
         def by_expert(dram):
             return dram.bitcast(I32).rearrange("e o p n -> p (e o) n")
 
-        for plane in (xs, w1s, wps, w2s):
+        for plane in (xs, wps, w1s, w2s):
             nc.vector.memset(plane[:].bitcast(I32), 0)
         nc.vector.memset(warm_in[:], 0.0)
         nc.scalar.activation(out=warm_out[:], in_=warm_in[:], func=GELU)
 
+        nc.gpsimd.dma_start(out=wpw[0][:].bitcast(I32), in_=by_expert(wp_words)[:, 0:2, :])
         make_identity(nc, ident[:])
 
         nc.sync.dma_start(offs_sb[:], offs)
-        nc.sync.dma_start(out=xw[:], in_=x_words.rearrange("o p t d -> p (o t d)").bitcast(I32))
-        load_scale_rows(nc, xs, x_scales.bitcast(I32).rearrange("o b t -> b (o t)"))
         nc.sync.dma_start(offs2_sb[:], offs2)
+        load_scale_rows(nc, xs, x_scales.bitcast(I32).rearrange("o b t -> b (o t)"))
+        nc.sync.dma_start(out=xw[:], in_=x_words.rearrange("o p t d -> p (o t d)").bitcast(I32))
+        load_scale_rows(nc, wps, by_expert(wp_scales), range(1))
         nc.sync.dma_start(out=w1w[0][:].bitcast(I32), in_=by_expert(w1_words)[:, 0:2, :])
-        nc.sync.dma_start(out=wpw[0][:].bitcast(I32), in_=by_expert(wp_words)[:, 0:2, :])
+        load_scale_rows(nc, wps, by_expert(wp_scales), range(1, 4))
         load_scale_rows(nc, w1s, by_expert(w1_scales))
-        load_scale_rows(nc, wps, by_expert(wp_scales))
         nc.sync.dma_start(out=w1w[1][:].bitcast(I32), in_=by_expert(w1_words)[:, 2:4, :])
         nc.sync.dma_start(out=wpw[1][:].bitcast(I32), in_=by_expert(wp_words)[:, 2:4, :])
         load_scale_rows(nc, w2s, by_expert(w2_scales))
@@ -85,32 +86,30 @@ def tile_moe_duo_gelu_kernel(
         nc.sync.dma_start(pos2_sb[:], pos2)
         nc.sync.dma_start(out=gates[:], in_=gate.rearrange("r p t -> p r t"))
 
-        gathered = []
-        for first, width in PIECES:
-            cols = slice(first // 16, (first + width) // 16)
+        grouped = [held("hq_in%d" % first, [P, width, 4], BF16) for first, width in RUNS]
+
+        def gather(s0):
+            cols = slice(s0 // 16, (s0 + P) // 16)
             sides = []
             for side, lst in enumerate((offs_sb, offs2_sb)):
-                words = held("gw%d_%d" % (first, side), [P, width], U32)
-                scales = held("gs%d_%d" % (first, side), [P, width], U8)
+                words = ring.tile([P, P], U32, name="gw%d" % side, align_bytes=64)
+                scales = ring.tile([P, P], U8, name="gs%d" % side, align_bytes=64)
                 nc.vector.tensor_copy(out=words[:], in_=xw[:].bitcast(U32).indirect(lst[:, cols]))
                 nc.vector.tensor_copy(out=scales[:], in_=xs[:].indirect(lst[:, cols]))
                 sides.append((words, scales))
-            gathered.append(sides)
+            return sides
 
-        grouped = []
-        for (first, width), sides in zip(PIECES, gathered):
-            e = first // C
-            hq_in = held("hq_in%d" % first, [P, width, 4], BF16)
-            grouped.append(hq_in)
-            for s0 in range(0, width, P):
-                cols = slice(s0, s0 + P)
+        for (first, width), hq_in in zip(RUNS, grouped):
+            for s0 in range(first, first + width, P):
+                e = s0 // C
+                sides = gather(s0)
                 pre = pre_banks.tile([P, H], F32, name="pre")
                 for side, (ww, ws) in enumerate(((w1w, w1s), (wpw, wps))):
                     words, scales = sides[side]
                     nc.tensor.matmul_mx(
                         out=pre[:],
-                        lhsT=words[:, cols].bitcast(FP8X4),
-                        lhsT_scale=scales[:, cols],
+                        lhsT=words[:].bitcast(FP8X4),
+                        lhsT_scale=scales[:],
                         rhs=ww[e // 2][:, e % 2, :].bitcast(FP4X4),
                         rhs_scale=ws[:, e, :],
                         start=(side == 0),
@@ -122,40 +121,42 @@ def tile_moe_duo_gelu_kernel(
                     in_=pre[:].rearrange("s (p u d) -> s u p d", u=2, d=2),
                     func=GELU,
                 )
-                turned = turn_banks.tile([P, 2, P], F32, name="turned")
+                turned = turn_banks.tile([P, 2, P], F32, name="turn")
                 for u in range(2):
                     nc.tensor.transpose(turned[:, u, :], h[:].bitcast(F32)[:, u * P : (u + 1) * P], ident[:])
-                nc.scalar.copy(out=hq_in[:, cols, :].bitcast(F32), in_=turned[:].rearrange("p u s -> p s u"))
+                nc.scalar.copy(
+                    out=hq_in[:, s0 - first : s0 - first + P, :].bitcast(F32), in_=turned[:].rearrange("p u s -> p s u")
+                )
 
         ys = [held("y%d" % half, [P, S], F32) for half in range(2)]
-        runs = ((0, 1), (2, 3), (4,))
-        for r, run in enumerate(runs):
-            base = PIECES[run[0]][0]
-            total = sum(PIECES[i][1] for i in run)
+        for r, (first, width) in enumerate(RUNS):
             if r < 2:
-                banks = [y_banks.tile([P, total], F32, name="yb%d_%d" % (r, half)) for half in range(2)]
+                banks = [pre_banks.tile([P, width], F32, name="pre"), turn_banks.tile([P, width], F32, name="turn")]
             else:
-                banks = [pre_banks.tile([P, total], F32, name="pre") for half in range(2)]
-            for i in run:
-                first, width = PIECES[i]
-                e = first // C
+                banks = [y_banks.tile([P, width], F32, name="yb%d_%d" % (r, half)) for half in range(2)]
+            if r == 0:
+                codes = ring.tile([P, width], U32, name="h", align_bytes=64)
+            else:
                 codes = held("hc%d" % first, [P, width], U32)
-                scales = held("hs%d" % first, [P, width], U8)
-                nc.vector.quantize_mx(
-                    out=codes[:].bitcast(FP8X4), scales=scales[:], in_=grouped[i][:].rearrange("p s d -> p (s d)")
-                )
-                for half in range(2):
+            scales = held("hs%d" % first, [P, width], U8)
+            nc.vector.quantize_mx(
+                out=codes[:].bitcast(FP8X4), scales=scales[:], in_=grouped[r][:].rearrange("p s d -> p (s d)")
+            )
+            for half in range(2):
+                for c0 in range(0, width, C):
+                    cols = slice(c0, min(c0 + C, width))
+                    e = (first + c0) // C
                     nc.tensor.matmul_mx(
-                        out=banks[half][:, first - base : first - base + width],
+                        out=banks[half][:, cols],
                         lhsT=w2w[:, e, 2 * P * half : 2 * P * (half + 1)].bitcast(FP4X4),
                         lhsT_scale=w2s[:, e, P * half : P * (half + 1)],
-                        rhs=codes[:].bitcast(FP8X4),
-                        rhs_scale=scales[:],
+                        rhs=codes[:, cols].bitcast(FP8X4),
+                        rhs_scale=scales[:, cols],
                         start=True,
                         stop=True,
                     )
-            nc.vector.tensor_copy(out=ys[0][:, base : base + total], in_=banks[0][:])
-            nc.scalar.copy(out=ys[1][:, base : base + total], in_=banks[1][:])
+            nc.vector.tensor_copy(out=ys[0][:, first : first + width], in_=banks[0][:])
+            nc.scalar.copy(out=ys[1][:, first : first + width], in_=banks[1][:])
 
         parts = [[held("part%d_%d" % (half, r), [P, T], F32) for r in range(2)] for half in range(2)]
         sums = [held("sum%d" % half, [P, T], F32) for half in range(2)]

@@ -20,12 +20,13 @@ GELU = mybir.ActivationFunctionType.Gelu_apprx_tanh
 MULT = mybir.AluOpType.mult
 ADD = mybir.AluOpType.add
 
+PIECES = ((0, 256), (256, 256), (512, 256), (768, 128), (896, 128))
 RUNS = ((0, 512), (512, 256), (768, 128), (896, 128))
 
 
-def load_scale_rows(nc, plane, rows, quadrants=range(4)):
+def load_scale_rows(queue, plane, rows, quadrants=range(4)):
     for q in quadrants:
-        nc.sync.dma_start(out=plane[32 * q : 32 * q + 4].bitcast(I32), in_=rows[4 * q : 4 * q + 4])
+        queue.dma_start(out=plane[32 * q : 32 * q + 4].bitcast(I32), in_=rows[4 * q : 4 * q + 4])
 
 
 def tile_moe_duo_gelu_kernel(
@@ -34,9 +35,10 @@ def tile_moe_duo_gelu_kernel(
     nc = tc.nc
     with ExitStack() as ctx:
         keep = ctx.enter_context(tc.tile_pool(name="keep", bufs=1))
-        ring = ctx.enter_context(tc.tile_pool(name="ring", bufs=3))
-        pre_banks = ctx.enter_context(tc.psum_pool(name="pre_banks", bufs=2))
-        turn_banks = ctx.enter_context(tc.psum_pool(name="turn_banks", bufs=2))
+        ring = ctx.enter_context(tc.tile_pool(name="ring", bufs=4))
+        pairs = ctx.enter_context(tc.tile_pool(name="pairs", bufs=2))
+        pre_banks = ctx.enter_context(tc.psum_pool(name="pre_banks", bufs=3))
+        turn_banks = ctx.enter_context(tc.psum_pool(name="turn_banks", bufs=3))
         y_banks = ctx.enter_context(tc.psum_pool(name="y_banks", bufs=1))
 
         def held(name, shape, dtype):
@@ -51,8 +53,8 @@ def tile_moe_duo_gelu_kernel(
         w1s = held("w1s", [P, E, H], U8)
         wps = held("wps", [P, E, H], U8)
         w2s = held("w2s", [P, E, N], U8)
-        w1w = [held("w1w%d" % a, [P, 2, 2 * H], U8) for a in range(2)]
-        wpw = [held("wpw%d" % a, [P, 2, 2 * H], U8) for a in range(2)]
+        w1w = held("w1w", [P, E, 2 * H], U8)
+        wpw = held("wpw", [P, E, 2 * H], U8)
         w2w = held("w2w", [P, E, 2 * N], U8)
         gates = held("gates", [P, 2, T], F32)
         ident = held("ident", [P, P], F32)
@@ -62,25 +64,32 @@ def tile_moe_duo_gelu_kernel(
         def by_expert(dram):
             return dram.bitcast(I32).rearrange("e o p n -> p (e o) n")
 
-        for plane in (xs, wps, w1s, w2s):
-            nc.vector.memset(plane[:].bitcast(I32), 0)
+        nc.vector.memset(xs[:].bitcast(I32), 0)
         nc.vector.memset(warm_in[:], 0.0)
-        nc.scalar.activation(out=warm_out[:], in_=warm_in[:], func=GELU)
+        for plane in (wps, w1s, w2s):
+            nc.vector.memset(plane[:].bitcast(I32), 0)
 
-        nc.gpsimd.dma_start(out=wpw[0][:].bitcast(I32), in_=by_expert(wp_words)[:, 0:2, :])
+        def load_words(queue, tile, dram, experts):
+            queue.dma_start(out=tile[:, experts, :].bitcast(I32), in_=by_expert(dram)[:, experts, :])
+
+        load_words(nc.gpsimd, wpw, wp_words, slice(0, 1))
         make_identity(nc, ident[:])
 
+        x_rows = x_scales.bitcast(I32).rearrange("o b t -> b (o t)")
         nc.sync.dma_start(offs_sb[:], offs)
-        nc.sync.dma_start(offs2_sb[:], offs2)
-        load_scale_rows(nc, xs, x_scales.bitcast(I32).rearrange("o b t -> b (o t)"))
+        load_scale_rows(nc.sync, xs, x_rows, range(2))
+        load_scale_rows(nc.scalar, xs, x_rows, range(2, 4))
+        nc.scalar.activation(out=warm_out[:], in_=warm_in[:], func=GELU)
         nc.sync.dma_start(out=xw[:], in_=x_words.rearrange("o p t d -> p (o t d)").bitcast(I32))
-        load_scale_rows(nc, wps, by_expert(wp_scales), range(1))
-        nc.sync.dma_start(out=w1w[0][:].bitcast(I32), in_=by_expert(w1_words)[:, 0:2, :])
-        load_scale_rows(nc, wps, by_expert(wp_scales), range(1, 4))
-        load_scale_rows(nc, w1s, by_expert(w1_scales))
-        nc.sync.dma_start(out=w1w[1][:].bitcast(I32), in_=by_expert(w1_words)[:, 2:4, :])
-        nc.sync.dma_start(out=wpw[1][:].bitcast(I32), in_=by_expert(wp_words)[:, 2:4, :])
-        load_scale_rows(nc, w2s, by_expert(w2_scales))
+        nc.sync.dma_start(offs2_sb[:], offs2)
+        load_scale_rows(nc.sync, wps, by_expert(wp_scales), range(1))
+        load_words(nc.sync, w1w, w1_words, slice(0, 1))
+        load_scale_rows(nc.sync, wps, by_expert(wp_scales), range(1, 4))
+        load_scale_rows(nc.scalar, w1s, by_expert(w1_scales))
+        for experts in (slice(1, 2), slice(2, 4)):
+            load_words(nc.sync, w1w, w1_words, experts)
+            load_words(nc.sync, wpw, wp_words, experts)
+        load_scale_rows(nc.sync, w2s, by_expert(w2_scales))
         nc.sync.dma_start(out=w2w[:].bitcast(I32), in_=by_expert(w2_words))
         nc.sync.dma_start(pos1_sb[:], pos1)
         nc.sync.dma_start(pos2_sb[:], pos2)
@@ -88,39 +97,46 @@ def tile_moe_duo_gelu_kernel(
 
         grouped = [held("hq_in%d" % first, [P, width, 4], BF16) for first, width in RUNS]
 
-        def gather(s0):
-            cols = slice(s0 // 16, (s0 + P) // 16)
+        gathered = {}
+
+        def gather(first, width):
+            cols = slice(first // 16, (first + width) // 16)
             sides = []
             for side, lst in enumerate((offs_sb, offs2_sb)):
-                words = ring.tile([P, P], U32, name="gw%d" % side, align_bytes=64)
-                scales = ring.tile([P, P], U8, name="gs%d" % side, align_bytes=64)
+                words = pairs.tile([P, width], U32, name="gw%d" % side, align_bytes=64)
+                scales = pairs.tile([P, width], U8, name="gs%d" % side, align_bytes=64)
                 nc.vector.tensor_copy(out=words[:], in_=xw[:].bitcast(U32).indirect(lst[:, cols]))
                 nc.vector.tensor_copy(out=scales[:], in_=xs[:].indirect(lst[:, cols]))
                 sides.append((words, scales))
-            return sides
+            for c0 in range(0, width, P):
+                gathered[first + c0] = [(w[:, c0 : c0 + P], s[:, c0 : c0 + P]) for w, s in sides]
 
         for (first, width), hq_in in zip(RUNS, grouped):
             for s0 in range(first, first + width, P):
                 e = s0 // C
-                sides = gather(s0)
+                if s0 in dict(PIECES):
+                    gather(s0, dict(PIECES)[s0])
+                sides = gathered[s0]
                 pre = pre_banks.tile([P, H], F32, name="pre")
                 for side, (ww, ws) in enumerate(((w1w, w1s), (wpw, wps))):
                     words, scales = sides[side]
                     nc.tensor.matmul_mx(
                         out=pre[:],
-                        lhsT=words[:].bitcast(FP8X4),
-                        lhsT_scale=scales[:],
-                        rhs=ww[e // 2][:, e % 2, :].bitcast(FP4X4),
+                        lhsT=words.bitcast(FP8X4),
+                        lhsT_scale=scales,
+                        rhs=ww[:, e, :].bitcast(FP4X4),
                         rhs_scale=ws[:, e, :],
                         start=(side == 0),
                         stop=(side == 1),
                     )
                 h = ring.tile([P, H], BF16, name="h", align_bytes=64)
-                nc.scalar.activation(
-                    out=h[:].rearrange("s (u p d) -> s u p d", u=2, d=2),
-                    in_=pre[:].rearrange("s (p u d) -> s u p d", u=2, d=2),
-                    func=GELU,
-                )
+                h_view = h[:].rearrange("s (u p d) -> s u p d", u=2, d=2)
+                pre_view = pre[:].rearrange("s (p u d) -> s u p d", u=2, d=2)
+                if s0 + P < S:
+                    nc.scalar.activation(out=h_view, in_=pre_view, func=GELU)
+                else:
+                    for u in range(2):
+                        nc.scalar.activation(out=h_view[:, u], in_=pre_view[:, u], func=GELU)
                 turned = turn_banks.tile([P, 2, P], F32, name="turn")
                 for u in range(2):
                     nc.tensor.transpose(turned[:, u, :], h[:].bitcast(F32)[:, u * P : (u + 1) * P], ident[:])
@@ -129,11 +145,24 @@ def tile_moe_duo_gelu_kernel(
                 )
 
         ys = [held("y%d" % half, [P, S], F32) for half in range(2)]
+
+        def project(half, bank, at, codes, scales, first, width):
+            for c0 in range(0, width, C):
+                cols = slice(c0, min(c0 + C, width))
+                e = (first + c0) // C
+                nc.tensor.matmul_mx(
+                    out=bank[:, at + cols.start : at + cols.stop],
+                    lhsT=w2w[:, e, 2 * P * half : 2 * P * (half + 1)].bitcast(FP4X4),
+                    lhsT_scale=w2s[:, e, P * half : P * (half + 1)],
+                    rhs=codes[:, cols].bitcast(FP8X4),
+                    rhs_scale=scales[:, cols],
+                    start=True,
+                    stop=True,
+                )
+
+        quantised = []
+        upper = None
         for r, (first, width) in enumerate(RUNS):
-            if r < 2:
-                banks = [pre_banks.tile([P, width], F32, name="pre"), turn_banks.tile([P, width], F32, name="turn")]
-            else:
-                banks = [y_banks.tile([P, width], F32, name="yb%d_%d" % (r, half)) for half in range(2)]
             if r == 0:
                 codes = ring.tile([P, width], U32, name="h", align_bytes=64)
             else:
@@ -142,21 +171,24 @@ def tile_moe_duo_gelu_kernel(
             nc.vector.quantize_mx(
                 out=codes[:].bitcast(FP8X4), scales=scales[:], in_=grouped[r][:].rearrange("p s d -> p (s d)")
             )
-            for half in range(2):
-                for c0 in range(0, width, C):
-                    cols = slice(c0, min(c0 + C, width))
-                    e = (first + c0) // C
-                    nc.tensor.matmul_mx(
-                        out=banks[half][:, cols],
-                        lhsT=w2w[:, e, 2 * P * half : 2 * P * (half + 1)].bitcast(FP4X4),
-                        lhsT_scale=w2s[:, e, P * half : P * (half + 1)],
-                        rhs=codes[:, cols].bitcast(FP8X4),
-                        rhs_scale=scales[:, cols],
-                        start=True,
-                        stop=True,
-                    )
-            nc.vector.tensor_copy(out=ys[0][:, first : first + width], in_=banks[0][:])
-            nc.scalar.copy(out=ys[1][:, first : first + width], in_=banks[1][:])
+            quantised.append((codes, scales, first, width))
+            if r < 3:
+                bank = pre_banks.tile([P, width], F32, name="pre")
+            else:
+                bank = y_banks.tile([P, width], F32, name="late")
+            project(0, bank, 0, *quantised[r])
+            if r < 2:
+                nc.vector.tensor_copy(out=ys[0][:, first : first + width], in_=bank[:])
+            else:
+                nc.scalar.copy(out=ys[0][:, first : first + width], in_=bank[:])
+            if r == 1:
+                upper = turn_banks.tile([P, S // 2], F32, name="turn")
+            if r >= 1:
+                project(1, upper, first - S // 2, *quantised[r])
+        nc.scalar.copy(out=ys[1][:, S // 2 :], in_=upper[:])
+        lower = turn_banks.tile([P, S // 2], F32, name="turn")
+        project(1, lower, 0, *quantised[0])
+        nc.scalar.copy(out=ys[1][:, : S // 2], in_=lower[:])
 
         parts = [[held("part%d_%d" % (half, r), [P, T], F32) for r in range(2)] for half in range(2)]
         sums = [held("sum%d" % half, [P, T], F32) for half in range(2)]
@@ -173,12 +205,9 @@ def tile_moe_duo_gelu_kernel(
 
         fetch(0, 0, 0, 512)
         fetch(0, 1, 0, 512)
-        fetch(1, 0, 0, 256)
+        fetch(1, 0, 0, 512)
         finish(0, 0, 512)
-        fetch(1, 1, 0, 256)
-        fetch(1, 0, 256, 512)
-        finish(1, 0, 256)
-        fetch(1, 1, 256, 384)
+        fetch(1, 1, 0, 384)
         fetch(1, 1, 384, 512)
-        finish(1, 256, 384)
+        finish(1, 0, 384)
         finish(1, 384, 512)

@@ -36,7 +36,6 @@ def tile_moe_duo_gelu_kernel(
     with ExitStack() as ctx:
         keep = ctx.enter_context(tc.tile_pool(name="keep", bufs=1))
         ring = ctx.enter_context(tc.tile_pool(name="ring", bufs=4))
-        pairs = ctx.enter_context(tc.tile_pool(name="pairs", bufs=2))
         pre_banks = ctx.enter_context(tc.psum_pool(name="pre_banks", bufs=3))
         turn_banks = ctx.enter_context(tc.psum_pool(name="turn_banks", bufs=3))
         y_banks = ctx.enter_context(tc.psum_pool(name="y_banks", bufs=1))
@@ -65,9 +64,9 @@ def tile_moe_duo_gelu_kernel(
             return dram.bitcast(I32).rearrange("e o p n -> p (e o) n")
 
         nc.vector.memset(xs[:].bitcast(I32), 0)
-        nc.vector.memset(warm_in[:], 0.0)
-        for plane in (wps, w1s, w2s):
+        for plane in (w1s, wps, w2s):
             nc.vector.memset(plane[:].bitcast(I32), 0)
+        nc.vector.memset(warm_in[:], 0.0)
 
         def load_words(queue, tile, dram, experts):
             queue.dma_start(out=tile[:, experts, :].bitcast(I32), in_=by_expert(dram)[:, experts, :])
@@ -76,16 +75,15 @@ def tile_moe_duo_gelu_kernel(
         make_identity(nc, ident[:])
 
         x_rows = x_scales.bitcast(I32).rearrange("o b t -> b (o t)")
-        nc.sync.dma_start(offs_sb[:], offs)
-        load_scale_rows(nc.sync, xs, x_rows, range(2))
-        load_scale_rows(nc.scalar, xs, x_rows, range(2, 4))
-        nc.scalar.activation(out=warm_out[:], in_=warm_in[:], func=GELU)
-        nc.sync.dma_start(out=xw[:], in_=x_words.rearrange("o p t d -> p (o t d)").bitcast(I32))
         nc.sync.dma_start(offs2_sb[:], offs2)
-        load_scale_rows(nc.sync, wps, by_expert(wp_scales), range(1))
-        load_words(nc.sync, w1w, w1_words, slice(0, 1))
-        load_scale_rows(nc.sync, wps, by_expert(wp_scales), range(1, 4))
+        nc.sync.dma_start(offs_sb[:], offs)
+        load_scale_rows(nc.sync, xs, x_rows, range(1))
+        load_scale_rows(nc.scalar, xs, x_rows, range(1, 4))
+        nc.sync.dma_start(out=xw[:], in_=x_words.rearrange("o p t d -> p (o t d)").bitcast(I32))
         load_scale_rows(nc.scalar, w1s, by_expert(w1_scales))
+        nc.scalar.activation(out=warm_out[:], in_=warm_in[:], func=GELU)
+        load_words(nc.sync, w1w, w1_words, slice(0, 1))
+        load_scale_rows(nc.sync, wps, by_expert(wp_scales))
         for experts in (slice(1, 2), slice(2, 4)):
             load_words(nc.sync, w1w, w1_words, experts)
             load_words(nc.sync, wpw, wp_words, experts)
@@ -102,9 +100,9 @@ def tile_moe_duo_gelu_kernel(
         def gather(first, width):
             cols = slice(first // 16, (first + width) // 16)
             sides = []
-            for side, lst in enumerate((offs_sb, offs2_sb)):
-                words = pairs.tile([P, width], U32, name="gw%d" % side, align_bytes=64)
-                scales = pairs.tile([P, width], U8, name="gs%d" % side, align_bytes=64)
+            for side, lst in enumerate((offs2_sb, offs_sb)):
+                words = held("gw%d_%d" % (first, side), [P, width], U32)
+                scales = held("gs%d_%d" % (first, side), [P, width], U8)
                 nc.vector.tensor_copy(out=words[:], in_=xw[:].bitcast(U32).indirect(lst[:, cols]))
                 nc.vector.tensor_copy(out=scales[:], in_=xs[:].indirect(lst[:, cols]))
                 sides.append((words, scales))
@@ -118,7 +116,7 @@ def tile_moe_duo_gelu_kernel(
                     gather(s0, dict(PIECES)[s0])
                 sides = gathered[s0]
                 pre = pre_banks.tile([P, H], F32, name="pre")
-                for side, (ww, ws) in enumerate(((w1w, w1s), (wpw, wps))):
+                for side, (ww, ws) in enumerate(((wpw, wps), (w1w, w1s))):
                     words, scales = sides[side]
                     nc.tensor.matmul_mx(
                         out=pre[:],
@@ -163,10 +161,7 @@ def tile_moe_duo_gelu_kernel(
         quantised = []
         upper = None
         for r, (first, width) in enumerate(RUNS):
-            if r == 0:
-                codes = ring.tile([P, width], U32, name="h", align_bytes=64)
-            else:
-                codes = held("hc%d" % first, [P, width], U32)
+            codes = held("hc%d" % first, [P, width], U32)
             scales = held("hs%d" % first, [P, width], U8)
             nc.vector.quantize_mx(
                 out=codes[:].bitcast(FP8X4), scales=scales[:], in_=grouped[r][:].rearrange("p s d -> p (s d)")
@@ -206,8 +201,9 @@ def tile_moe_duo_gelu_kernel(
         fetch(0, 0, 0, 512)
         fetch(0, 1, 0, 512)
         fetch(1, 0, 0, 512)
-        finish(0, 0, 512)
         fetch(1, 1, 0, 384)
-        fetch(1, 1, 384, 512)
+        finish(0, 0, 384)
         finish(1, 0, 384)
+        fetch(1, 1, 384, 512)
+        finish(0, 384, 512)
         finish(1, 384, 512)

@@ -63,7 +63,7 @@ def tile_moe_duo_gelu_kernel(
         def by_expert(dram):
             return dram.bitcast(I32).rearrange("e o p n -> p (e o) n")
 
-        nc.vector.memset(xs[:].bitcast(I32), 0)
+        nc.gpsimd.memset(xs[:].bitcast(I32), 0)
         for plane in (w1s, wps, w2s):
             nc.vector.memset(plane[:].bitcast(I32), 0)
         nc.vector.memset(warm_in[:], 0.0)

@@ -36,8 +36,8 @@ def tile_moe_duo_gelu_kernel(
     with ExitStack() as ctx:
         keep = ctx.enter_context(tc.tile_pool(name="keep", bufs=1))
         ring = ctx.enter_context(tc.tile_pool(name="ring", bufs=4))
-        pre_banks = ctx.enter_context(tc.psum_pool(name="pre_banks", bufs=3))
-        turn_banks = ctx.enter_context(tc.psum_pool(name="turn_banks", bufs=3))
+        pre_banks = ctx.enter_context(tc.psum_pool(name="pre_banks", bufs=2))
+        turn_banks = ctx.enter_context(tc.psum_pool(name="turn_banks", bufs=2))
         y_banks = ctx.enter_context(tc.psum_pool(name="y_banks", bufs=1))
 
         def held(name, shape, dtype):
@@ -63,30 +63,38 @@ def tile_moe_duo_gelu_kernel(
         def by_expert(dram):
             return dram.bitcast(I32).rearrange("e o p n -> p (e o) n")
 
-        nc.gpsimd.memset(xs[:].bitcast(I32), 0)
-        for plane in (w1s, wps, w2s):
+        nc.gpsimd.memset(warm_in[:], 0.0)
+        for plane in (w1s, wps):
             nc.vector.memset(plane[:].bitcast(I32), 0)
-        nc.vector.memset(warm_in[:], 0.0)
+        nc.vector.memset(ident[:], 0.0)
+        nc.vector.memset(w2s[:].bitcast(I32), 0)
 
         def load_words(queue, tile, dram, experts):
             queue.dma_start(out=tile[:, experts, :].bitcast(I32), in_=by_expert(dram)[:, experts, :])
 
         load_words(nc.gpsimd, wpw, wp_words, slice(0, 1))
-        make_identity(nc, ident[:])
+        make_identity(nc, ident[:], nomemset=True)
 
         x_rows = x_scales.bitcast(I32).rearrange("o b t -> b (o t)")
+
+        def load_token_scales(queue, q):
+            rows = x_rows[4 * q : 4 * q + 4].unsqueeze(0).broadcast_to([8, 4, T // 4])
+            queue.dma_start(out=xs[32 * q : 32 * q + 32].bitcast(I32), in_=rows)
+
         nc.sync.dma_start(offs2_sb[:], offs2)
         nc.sync.dma_start(offs_sb[:], offs)
-        load_scale_rows(nc.sync, xs, x_rows, range(1))
-        load_scale_rows(nc.scalar, xs, x_rows, range(1, 4))
-        nc.sync.dma_start(out=xw[:], in_=x_words.rearrange("o p t d -> p (o t d)").bitcast(I32))
-        load_scale_rows(nc.scalar, w1s, by_expert(w1_scales))
-        nc.scalar.activation(out=warm_out[:], in_=warm_in[:], func=GELU)
+        for q in range(3):
+            load_token_scales(nc.scalar, q)
         load_words(nc.sync, w1w, w1_words, slice(0, 1))
-        load_scale_rows(nc.sync, wps, by_expert(wp_scales))
+        load_token_scales(nc.sync, 3)
+        nc.scalar.dma_start(out=xw[:], in_=x_words.rearrange("o p t d -> p (o t d)").bitcast(I32))
+        nc.scalar.activation(out=warm_out[:], in_=warm_in[:], func=GELU)
+        load_scale_rows(nc.sync, w1s, by_expert(w1_scales))
+        load_scale_rows(nc.sync, wps, by_expert(wp_scales), range(1))
+        load_scale_rows(nc.scalar, wps, by_expert(wp_scales), range(1, 4))
         for experts in (slice(1, 2), slice(2, 4)):
-            load_words(nc.sync, w1w, w1_words, experts)
             load_words(nc.sync, wpw, wp_words, experts)
+            load_words(nc.sync, w1w, w1_words, experts)
         load_scale_rows(nc.sync, w2s, by_expert(w2_scales))
         nc.sync.dma_start(out=w2w[:].bitcast(I32), in_=by_expert(w2_words))
         nc.sync.dma_start(pos1_sb[:], pos1)
@@ -99,48 +107,60 @@ def tile_moe_duo_gelu_kernel(
 
         def gather(first, width):
             cols = slice(first // 16, (first + width) // 16)
-            sides = []
-            for side, lst in enumerate((offs2_sb, offs_sb)):
-                words = held("gw%d_%d" % (first, side), [P, width], U32)
-                scales = held("gs%d_%d" % (first, side), [P, width], U8)
-                nc.vector.tensor_copy(out=words[:], in_=xw[:].bitcast(U32).indirect(lst[:, cols]))
-                nc.vector.tensor_copy(out=scales[:], in_=xs[:].indirect(lst[:, cols]))
-                sides.append((words, scales))
+            sides = [
+                (held("gw%d_%d" % (first, side), [P, width], U32), held("gs%d_%d" % (first, side), [P, width], U8))
+                for side in range(2)
+            ]
+            windows = (xw[:].bitcast(U32), xs[:])
+            order = ((0, 1), (1, 1), (0, 0), (1, 0)) if first == 0 else ((0, 0), (0, 1), (1, 0), (1, 1))
+            for side, sort in order:
+                lst = (offs2_sb, offs_sb)[side]
+                nc.vector.tensor_copy(out=sides[side][sort][:], in_=windows[sort].indirect(lst[:, cols]))
             for c0 in range(0, width, P):
                 gathered[first + c0] = [(w[:, c0 : c0 + P], s[:, c0 : c0 + P]) for w, s in sides]
 
-        for (first, width), hq_in in zip(RUNS, grouped):
-            for s0 in range(first, first + width, P):
-                e = s0 // C
-                if s0 in dict(PIECES):
-                    gather(s0, dict(PIECES)[s0])
-                sides = gathered[s0]
-                pre = pre_banks.tile([P, H], F32, name="pre")
-                for side, (ww, ws) in enumerate(((wpw, wps), (w1w, w1s))):
-                    words, scales = sides[side]
-                    nc.tensor.matmul_mx(
-                        out=pre[:],
-                        lhsT=words.bitcast(FP8X4),
-                        lhsT_scale=scales,
-                        rhs=ww[:, e, :].bitcast(FP4X4),
-                        rhs_scale=ws[:, e, :],
-                        start=(side == 0),
-                        stop=(side == 1),
-                    )
-                h = ring.tile([P, H], BF16, name="h", align_bytes=64)
-                h_view = h[:].rearrange("s (u p d) -> s u p d", u=2, d=2)
-                pre_view = pre[:].rearrange("s (p u d) -> s u p d", u=2, d=2)
-                if s0 + P < S:
-                    nc.scalar.activation(out=h_view, in_=pre_view, func=GELU)
-                else:
-                    for u in range(2):
-                        nc.scalar.activation(out=h_view[:, u], in_=pre_view[:, u], func=GELU)
-                turned = turn_banks.tile([P, 2, P], F32, name="turn")
-                for u in range(2):
-                    nc.tensor.transpose(turned[:, u, :], h[:].bitcast(F32)[:, u * P : (u + 1) * P], ident[:])
-                nc.scalar.copy(
-                    out=hq_in[:, s0 - first : s0 - first + P, :].bitcast(F32), in_=turned[:].rearrange("p u s -> p s u")
+        hidden = {}
+
+        def first_layer(s0):
+            e = s0 // C
+            if s0 in dict(PIECES):
+                gather(s0, dict(PIECES)[s0])
+            sides = gathered[s0]
+            pre = pre_banks.tile([P, H], F32, name="pre")
+            for side, (ww, ws) in enumerate(((wpw, wps), (w1w, w1s))):
+                words, scales = sides[side]
+                nc.tensor.matmul_mx(
+                    out=pre[:],
+                    lhsT=words.bitcast(FP8X4),
+                    lhsT_scale=scales,
+                    rhs=ww[:, e, :].bitcast(FP4X4),
+                    rhs_scale=ws[:, e, :],
+                    start=(side == 0),
+                    stop=(side == 1),
                 )
+            h = ring.tile([P, H], BF16, name="h", align_bytes=64)
+            h_view = h[:].rearrange("s (u p d) -> s u p d", u=2, d=2)
+            pre_view = pre[:].rearrange("s (p u d) -> s u p d", u=2, d=2)
+            if s0 + P < S:
+                nc.scalar.activation(out=h_view, in_=pre_view, func=GELU)
+            else:
+                for u in range(2):
+                    nc.scalar.activation(out=h_view[:, u], in_=pre_view[:, u], func=GELU)
+            hidden[s0] = h
+
+        def turn(s0):
+            (first, hq_in), = [(f, g) for (f, w), g in zip(RUNS, grouped) if f <= s0 < f + w]
+            turned = turn_banks.tile([P, 2, P], F32, name="turn")
+            for u in range(2):
+                nc.tensor.transpose(turned[:, u, :], hidden[s0][:].bitcast(F32)[:, u * P : (u + 1) * P], ident[:])
+            move = nc.vector.tensor_copy if s0 == S - 2 * P else nc.scalar.copy
+            move(out=hq_in[:, s0 - first : s0 - first + P, :].bitcast(F32), in_=turned[:].rearrange("p u s -> p s u"))
+
+        for s0 in range(0, S + 1 * P, P):
+            if s0 < S:
+                first_layer(s0)
+            if s0 >= 1 * P:
+                turn(s0 - 1 * P)
 
         ys = [held("y%d" % half, [P, S], F32) for half in range(2)]
 
@@ -159,7 +179,6 @@ def tile_moe_duo_gelu_kernel(
                 )
 
         quantised = []
-        upper = None
         for r, (first, width) in enumerate(RUNS):
             codes = held("hc%d" % first, [P, width], U32)
             scales = held("hs%d" % first, [P, width], U8)
@@ -167,23 +186,20 @@ def tile_moe_duo_gelu_kernel(
                 out=codes[:].bitcast(FP8X4), scales=scales[:], in_=grouped[r][:].rearrange("p s d -> p (s d)")
             )
             quantised.append((codes, scales, first, width))
-            if r < 3:
+            if r < 2:
                 bank = pre_banks.tile([P, width], F32, name="pre")
             else:
-                bank = y_banks.tile([P, width], F32, name="late")
+                bank = y_banks.tile([P, width], F32, name="late%d" % r)
             project(0, bank, 0, *quantised[r])
-            if r < 2:
-                nc.vector.tensor_copy(out=ys[0][:, first : first + width], in_=bank[:])
-            else:
-                nc.scalar.copy(out=ys[0][:, first : first + width], in_=bank[:])
-            if r == 1:
-                upper = turn_banks.tile([P, S // 2], F32, name="turn")
-            if r >= 1:
-                project(1, upper, first - S // 2, *quantised[r])
-        nc.scalar.copy(out=ys[1][:, S // 2 :], in_=upper[:])
+            move = nc.scalar.copy if r == 1 else nc.vector.tensor_copy
+            move(out=ys[0][:, first : first + width], in_=bank[:])
+        upper = turn_banks.tile([P, S // 2], F32, name="turn")
         lower = turn_banks.tile([P, S // 2], F32, name="turn")
         project(1, lower, 0, *quantised[0])
         nc.scalar.copy(out=ys[1][:, : S // 2], in_=lower[:])
+        for run in quantised[1:]:
+            project(1, upper, run[2] - S // 2, *run)
+        nc.scalar.copy(out=ys[1][:, S // 2 :], in_=upper[:])
 
         parts = [[held("part%d_%d" % (half, r), [P, T], F32) for r in range(2)] for half in range(2)]
         sums = [held("sum%d" % half, [P, T], F32) for half in range(2)]

@@ -20,7 +20,6 @@ GELU = mybir.ActivationFunctionType.Gelu_apprx_tanh
 MULT = mybir.AluOpType.mult
 ADD = mybir.AluOpType.add
 
-PIECES = ((0, 256), (256, 256), (512, 256), (768, 128), (896, 128))
 RUNS = ((0, 512), (512, 256), (768, 128), (896, 128))
 
 
@@ -64,7 +63,7 @@ def tile_moe_duo_gelu_kernel(
             return dram.bitcast(I32).rearrange("e o p n -> p (e o) n")
 
         nc.gpsimd.memset(warm_in[:], 0.0)
-        for plane in (w1s, wps):
+        for plane in (wps, w1s):
             nc.vector.memset(plane[:].bitcast(I32), 0)
         nc.vector.memset(ident[:], 0.0)
         nc.vector.memset(w2s[:].bitcast(I32), 0)
@@ -88,10 +87,10 @@ def tile_moe_duo_gelu_kernel(
         load_words(nc.sync, w1w, w1_words, slice(0, 1))
         load_token_scales(nc.sync, 3)
         nc.scalar.dma_start(out=xw[:], in_=x_words.rearrange("o p t d -> p (o t d)").bitcast(I32))
+        for plane, rows in ((wps, wp_scales), (w1s, w1_scales)):
+            load_scale_rows(nc.sync, plane, by_expert(rows), range(2))
+            load_scale_rows(nc.scalar, plane, by_expert(rows), range(2, 4))
         nc.scalar.activation(out=warm_out[:], in_=warm_in[:], func=GELU)
-        load_scale_rows(nc.sync, w1s, by_expert(w1_scales))
-        load_scale_rows(nc.sync, wps, by_expert(wp_scales), range(1))
-        load_scale_rows(nc.scalar, wps, by_expert(wp_scales), range(1, 4))
         for experts in (slice(1, 2), slice(2, 4)):
             load_words(nc.sync, wpw, wp_words, experts)
             load_words(nc.sync, w1w, w1_words, experts)
@@ -105,30 +104,37 @@ def tile_moe_duo_gelu_kernel(
 
         gathered = {}
 
-        def gather(first, width):
+        windows = (xw[:].bitcast(U32), xs[:])
+        lists = (offs2_sb, offs_sb)
+
+        def gather(side, sort, first, width):
+            tile = held("g%d_%d_%d" % (side, sort, first), [P, width], (U32, U8)[sort])
             cols = slice(first // 16, (first + width) // 16)
-            sides = [
-                (held("gw%d_%d" % (first, side), [P, width], U32), held("gs%d_%d" % (first, side), [P, width], U8))
-                for side in range(2)
-            ]
-            windows = (xw[:].bitcast(U32), xs[:])
-            order = ((0, 1), (1, 1), (0, 0), (1, 0)) if first == 0 else ((0, 0), (0, 1), (1, 0), (1, 1))
-            for side, sort in order:
-                lst = (offs2_sb, offs_sb)[side]
-                nc.vector.tensor_copy(out=sides[side][sort][:], in_=windows[sort].indirect(lst[:, cols]))
+            nc.vector.tensor_copy(out=tile[:], in_=windows[sort].indirect(lists[side][:, cols]))
             for c0 in range(0, width, P):
-                gathered[first + c0] = [(w[:, c0 : c0 + P], s[:, c0 : c0 + P]) for w, s in sides]
+                gathered[side, sort, first + c0] = tile[:, c0 : c0 + P]
+
+        for side in range(2):
+            gather(side, 1, 0, 2 * P)
+            gather(side, 0, 0, 2 * P)
+        for first in (2 * P, 4 * P):
+            for side in range(2):
+                gather(side, 1, first, 2 * P)
+                gather(side, 0, first, P)
+            for side in range(2):
+                gather(side, 0, first + P, P)
+        for first in (6 * P, 7 * P):
+            for side in range(2):
+                gather(side, 0, first, P)
+                gather(side, 1, first, P)
 
         hidden = {}
 
         def first_layer(s0):
             e = s0 // C
-            if s0 in dict(PIECES):
-                gather(s0, dict(PIECES)[s0])
-            sides = gathered[s0]
             pre = pre_banks.tile([P, H], F32, name="pre")
             for side, (ww, ws) in enumerate(((wpw, wps), (w1w, w1s))):
-                words, scales = sides[side]
+                words, scales = gathered[side, 0, s0], gathered[side, 1, s0]
                 nc.tensor.matmul_mx(
                     out=pre[:],
                     lhsT=words.bitcast(FP8X4),
@@ -203,23 +209,24 @@ def tile_moe_duo_gelu_kernel(
 
         parts = [[held("part%d_%d" % (half, r), [P, T], F32) for r in range(2)] for half in range(2)]
         sums = [held("sum%d" % half, [P, T], F32) for half in range(2)]
-        lists = (pos1_sb, pos2_sb)
+        places = (pos1_sb, pos2_sb)
 
         def fetch(half, r, t0, t1):
             nc.vector.tensor_tensor(
-                parts[half][r][:, t0:t1], ys[half][:].indirect(lists[r][:, t0 // 16 : t1 // 16]), gates[:, r, t0:t1], MULT
+                parts[half][r][:, t0:t1], ys[half][:].indirect(places[r][:, t0 // 16 : t1 // 16]), gates[:, r, t0:t1], MULT
             )
 
         def finish(half, t0, t1):
             nc.vector.tensor_tensor(sums[half][:, t0:t1], parts[half][0][:, t0:t1], parts[half][1][:, t0:t1], ADD)
             nc.sync.dma_start(out=out[P * half : P * (half + 1), t0:t1], in_=sums[half][:, t0:t1])
 
-        fetch(0, 0, 0, 512)
-        fetch(0, 1, 0, 512)
-        fetch(1, 0, 0, 512)
-        fetch(1, 1, 0, 384)
-        finish(0, 0, 384)
-        finish(1, 0, 384)
-        fetch(1, 1, 384, 512)
-        finish(0, 384, 512)
-        finish(1, 384, 512)
+        fetch(0, 0, 0, T)
+        fetch(0, 1, 0, T)
+        fetch(1, 0, 0, T)
+        finish(0, 0, T)
+        fetch(1, 1, 0, 2 * P)
+        fetch(1, 1, 2 * P, 3 * P)
+        finish(1, 0, 2 * P)
+        fetch(1, 1, 3 * P, T)
+        finish(1, 2 * P, 3 * P)
+        finish(1, 3 * P, T)

@@ -63,7 +63,7 @@ def tile_moe_duo_gelu_kernel(
             return dram.bitcast(I32).rearrange("e o p n -> p (e o) n")
 
         nc.gpsimd.memset(warm_in[:], 0.0)
-        for plane in (wps, w1s):
+        for plane in (w1s, wps):
             nc.vector.memset(plane[:].bitcast(I32), 0)
         nc.vector.memset(ident[:], 0.0)
         nc.vector.memset(w2s[:].bitcast(I32), 0)
@@ -87,10 +87,10 @@ def tile_moe_duo_gelu_kernel(
         load_words(nc.sync, w1w, w1_words, slice(0, 1))
         load_token_scales(nc.sync, 3)
         nc.scalar.dma_start(out=xw[:], in_=x_words.rearrange("o p t d -> p (o t d)").bitcast(I32))
-        for plane, rows in ((wps, wp_scales), (w1s, w1_scales)):
-            load_scale_rows(nc.sync, plane, by_expert(rows), range(2))
-            load_scale_rows(nc.scalar, plane, by_expert(rows), range(2, 4))
         nc.scalar.activation(out=warm_out[:], in_=warm_in[:], func=GELU)
+        load_scale_rows(nc.sync, w1s, by_expert(w1_scales))
+        load_scale_rows(nc.sync, wps, by_expert(wp_scales), range(1))
+        load_scale_rows(nc.scalar, wps, by_expert(wp_scales), range(1, 4))
         for experts in (slice(1, 2), slice(2, 4)):
             load_words(nc.sync, wpw, wp_words, experts)
             load_words(nc.sync, w1w, w1_words, experts)
@@ -115,18 +115,14 @@ def tile_moe_duo_gelu_kernel(
                 gathered[side, sort, first + c0] = tile[:, c0 : c0 + P]
 
         for side in range(2):
-            gather(side, 1, 0, 2 * P)
-            gather(side, 0, 0, 2 * P)
-        for first in (2 * P, 4 * P):
+            gather(side, 1, 0, 3 * P)
+        for first, width in ((0, P), (P, 2 * P)):
             for side in range(2):
-                gather(side, 1, first, 2 * P)
-                gather(side, 0, first, P)
+                gather(side, 0, first, width)
+        for first, width in ((3 * P, 2 * P), (5 * P, P), (6 * P, P), (7 * P, P)):
             for side in range(2):
-                gather(side, 0, first + P, P)
-        for first in (6 * P, 7 * P):
-            for side in range(2):
-                gather(side, 0, first, P)
-                gather(side, 1, first, P)
+                gather(side, 0, first, width)
+                gather(side, 1, first, width)
 
         hidden = {}
 
@@ -162,11 +158,15 @@ def tile_moe_duo_gelu_kernel(
             move = nc.vector.tensor_copy if s0 == S - 2 * P else nc.scalar.copy
             move(out=hq_in[:, s0 - first : s0 - first + P, :].bitcast(F32), in_=turned[:].rearrange("p u s -> p s u"))
 
-        for s0 in range(0, S + 1 * P, P):
-            if s0 < S:
-                first_layer(s0)
-            if s0 >= 1 * P:
-                turn(s0 - 1 * P)
+        waiting = []
+        for group in ((0,), (1, 2), (3, 4), (5,), (6,), (7,)):
+            for block in group:
+                first_layer(block * P)
+            waiting.extend(group)
+            for block in waiting[:-1]:
+                turn(block * P)
+            waiting = waiting[-1:]
+        turn(S - P)
 
         ys = [held("y%d" % half, [P, S], F32) for half in range(2)]
 
@@ -197,15 +197,15 @@ def tile_moe_duo_gelu_kernel(
             else:
                 bank = y_banks.tile([P, width], F32, name="late%d" % r)
             project(0, bank, 0, *quantised[r])
-            move = nc.scalar.copy if r == 1 else nc.vector.tensor_copy
+            move = nc.scalar.copy if r % 2 else nc.vector.tensor_copy
             move(out=ys[0][:, first : first + width], in_=bank[:])
         upper = turn_banks.tile([P, S // 2], F32, name="turn")
-        lower = turn_banks.tile([P, S // 2], F32, name="turn")
-        project(1, lower, 0, *quantised[0])
-        nc.scalar.copy(out=ys[1][:, : S // 2], in_=lower[:])
         for run in quantised[1:]:
             project(1, upper, run[2] - S // 2, *run)
         nc.scalar.copy(out=ys[1][:, S // 2 :], in_=upper[:])
+        lower = y_banks.tile([P, S // 2], F32, name="late3")
+        project(1, lower, 0, *quantised[0])
+        nc.scalar.copy(out=ys[1][:, : S // 2], in_=lower[:])
 
         parts = [[held("part%d_%d" % (half, r), [P, T], F32) for r in range(2)] for half in range(2)]
         sums = [held("sum%d" % half, [P, T], F32) for half in range(2)]

@@ -20,6 +20,11 @@ GELU = mybir.ActivationFunctionType.Gelu_apprx_tanh
 MULT = mybir.AluOpType.mult
 ADD = mybir.AluOpType.add
 
+PARTNER, TOKEN = 0, 1
+WORDS, SCALES = 0, 1
+LAST = S - P
+
+GROUPS = ((0,), (1, 2), (3, 4), (5, 6), (7,))
 RUNS = ((0, 512), (512, 256), (768, 128), (896, 128))
 
 
@@ -37,7 +42,7 @@ def tile_moe_duo_gelu_kernel(
         ring = ctx.enter_context(tc.tile_pool(name="ring", bufs=4))
         pre_banks = ctx.enter_context(tc.psum_pool(name="pre_banks", bufs=2))
         turn_banks = ctx.enter_context(tc.psum_pool(name="turn_banks", bufs=2))
-        y_banks = ctx.enter_context(tc.psum_pool(name="y_banks", bufs=1))
+        end_banks = ctx.enter_context(tc.psum_pool(name="end_banks", bufs=1))
 
         def held(name, shape, dtype):
             return keep.tile(shape, dtype, name=name, align_bytes=64)
@@ -80,11 +85,11 @@ def tile_moe_duo_gelu_kernel(
             rows = x_rows[4 * q : 4 * q + 4].unsqueeze(0).broadcast_to([8, 4, T // 4])
             queue.dma_start(out=xs[32 * q : 32 * q + 32].bitcast(I32), in_=rows)
 
+        load_words(nc.sync, w1w, w1_words, slice(0, 1))
         nc.sync.dma_start(offs2_sb[:], offs2)
         nc.sync.dma_start(offs_sb[:], offs)
         for q in range(3):
             load_token_scales(nc.scalar, q)
-        load_words(nc.sync, w1w, w1_words, slice(0, 1))
         load_token_scales(nc.sync, 3)
         nc.scalar.dma_start(out=xw[:], in_=x_words.rearrange("o p t d -> p (o t d)").bitcast(I32))
         nc.scalar.activation(out=warm_out[:], in_=warm_in[:], func=GELU)
@@ -100,10 +105,9 @@ def tile_moe_duo_gelu_kernel(
         nc.sync.dma_start(pos2_sb[:], pos2)
         nc.sync.dma_start(out=gates[:], in_=gate.rearrange("r p t -> p r t"))
 
-        grouped = [held("hq_in%d" % first, [P, width, 4], BF16) for first, width in RUNS]
+        h_turned = [held("h_turned%d" % first, [P, width, 4], BF16) for first, width in RUNS]
 
         gathered = {}
-
         windows = (xw[:].bitcast(U32), xs[:])
         lists = (offs2_sb, offs_sb)
 
@@ -114,36 +118,42 @@ def tile_moe_duo_gelu_kernel(
             for c0 in range(0, width, P):
                 gathered[side, sort, first + c0] = tile[:, c0 : c0 + P]
 
-        for side in range(2):
-            gather(side, 1, 0, 3 * P)
-        for first, width in ((0, P), (P, 2 * P)):
-            for side in range(2):
-                gather(side, 0, first, width)
-        for first, width in ((3 * P, 2 * P), (5 * P, P), (6 * P, P), (7 * P, P)):
-            for side in range(2):
-                gather(side, 0, first, width)
-                gather(side, 1, first, width)
+        def scales_then_words(first, early, late):
+            for side in (PARTNER, TOKEN):
+                gather(side, SCALES, first, early + late)
+            for start, width in ((first, early), (first + early, late)):
+                for side in (PARTNER, TOKEN):
+                    gather(side, WORDS, start, width)
+
+        def side_after_side(first, width):
+            for side in (PARTNER, TOKEN):
+                gather(side, WORDS, first, width)
+                gather(side, SCALES, first, width)
+
+        scales_then_words(0, P, 2 * P)
+        side_after_side(3 * P, 2 * P)
+        scales_then_words(5 * P, P, P)
+        side_after_side(LAST, P)
 
         hidden = {}
 
         def first_layer(s0):
             e = s0 // C
             pre = pre_banks.tile([P, H], F32, name="pre")
-            for side, (ww, ws) in enumerate(((wpw, wps), (w1w, w1s))):
-                words, scales = gathered[side, 0, s0], gathered[side, 1, s0]
+            for side, (ww, ws) in ((PARTNER, (wpw, wps)), (TOKEN, (w1w, w1s))):
                 nc.tensor.matmul_mx(
                     out=pre[:],
-                    lhsT=words.bitcast(FP8X4),
-                    lhsT_scale=scales,
+                    lhsT=gathered[side, WORDS, s0].bitcast(FP8X4),
+                    lhsT_scale=gathered[side, SCALES, s0],
                     rhs=ww[:, e, :].bitcast(FP4X4),
                     rhs_scale=ws[:, e, :],
-                    start=(side == 0),
-                    stop=(side == 1),
+                    start=(side == PARTNER),
+                    stop=(side == TOKEN),
                 )
             h = ring.tile([P, H], BF16, name="h", align_bytes=64)
             h_view = h[:].rearrange("s (u p d) -> s u p d", u=2, d=2)
             pre_view = pre[:].rearrange("s (p u d) -> s u p d", u=2, d=2)
-            if s0 + P < S:
+            if s0 < LAST:
                 nc.scalar.activation(out=h_view, in_=pre_view, func=GELU)
             else:
                 for u in range(2):
@@ -151,26 +161,29 @@ def tile_moe_duo_gelu_kernel(
             hidden[s0] = h
 
         def turn(s0):
-            (first, hq_in), = [(f, g) for (f, w), g in zip(RUNS, grouped) if f <= s0 < f + w]
-            turned = turn_banks.tile([P, 2, P], F32, name="turn")
+            ((first, target),) = [(f, tile) for (f, w), tile in zip(RUNS, h_turned) if f <= s0 < f + w]
+            if s0 < LAST:
+                turned = turn_banks.tile([P, 2, P], F32, name="turn")
+            else:
+                turned = end_banks.tile([P, 2, P], F32, name="last_turn")
             for u in range(2):
                 nc.tensor.transpose(turned[:, u, :], hidden[s0][:].bitcast(F32)[:, u * P : (u + 1) * P], ident[:])
-            move = nc.vector.tensor_copy if s0 == S - 2 * P else nc.scalar.copy
-            move(out=hq_in[:, s0 - first : s0 - first + P, :].bitcast(F32), in_=turned[:].rearrange("p u s -> p s u"))
+            move = nc.vector.tensor_copy if LAST - 2 * P <= s0 < LAST else nc.scalar.copy
+            move(out=target[:, s0 - first : s0 - first + P, :].bitcast(F32), in_=turned[:].rearrange("p u s -> p s u"))
 
         waiting = []
-        for group in ((0,), (1, 2), (3, 4), (5,), (6,), (7,)):
+        for group in GROUPS:
             for block in group:
                 first_layer(block * P)
             waiting.extend(group)
             for block in waiting[:-1]:
                 turn(block * P)
             waiting = waiting[-1:]
-        turn(S - P)
+        turn(LAST)
 
-        ys = [held("y%d" % half, [P, S], F32) for half in range(2)]
+        y = [held("y%d" % half, [P, S], F32) for half in range(2)]
 
-        def project(half, bank, at, codes, scales, first, width):
+        def second_layer(half, bank, at, codes, scales, first, width):
             for c0 in range(0, width, C):
                 cols = slice(c0, min(c0 + C, width))
                 e = (first + c0) // C
@@ -189,23 +202,23 @@ def tile_moe_duo_gelu_kernel(
             codes = held("hc%d" % first, [P, width], U32)
             scales = held("hs%d" % first, [P, width], U8)
             nc.vector.quantize_mx(
-                out=codes[:].bitcast(FP8X4), scales=scales[:], in_=grouped[r][:].rearrange("p s d -> p (s d)")
+                out=codes[:].bitcast(FP8X4), scales=scales[:], in_=h_turned[r][:].rearrange("p s d -> p (s d)")
             )
             quantised.append((codes, scales, first, width))
-            if r < 2:
+            if width > P:
                 bank = pre_banks.tile([P, width], F32, name="pre")
             else:
-                bank = y_banks.tile([P, width], F32, name="late%d" % r)
-            project(0, bank, 0, *quantised[r])
+                bank = end_banks.tile([P, width], F32, name="y_from%d" % first)
+            second_layer(0, bank, 0, *quantised[r])
             move = nc.scalar.copy if r % 2 else nc.vector.tensor_copy
-            move(out=ys[0][:, first : first + width], in_=bank[:])
-        upper = turn_banks.tile([P, S // 2], F32, name="turn")
-        for run in quantised[1:]:
-            project(1, upper, run[2] - S // 2, *run)
-        nc.scalar.copy(out=ys[1][:, S // 2 :], in_=upper[:])
-        lower = y_banks.tile([P, S // 2], F32, name="late3")
-        project(1, lower, 0, *quantised[0])
-        nc.scalar.copy(out=ys[1][:, : S // 2], in_=lower[:])
+            move(out=y[0][:, first : first + width], in_=bank[:])
+        upper = end_banks.tile([P, S // 2], F32, name="last_turn")
+        for codes, scales, first, width in quantised[1:]:
+            second_layer(1, upper, first - S // 2, codes, scales, first, width)
+        nc.scalar.copy(out=y[1][:, S // 2 :], in_=upper[:])
+        lower = end_banks.tile([P, S // 2], F32, name="y_from%d" % LAST)
+        second_layer(1, lower, 0, *quantised[0])
+        nc.scalar.copy(out=y[1][:, : S // 2], in_=lower[:])
 
         parts = [[held("part%d_%d" % (half, r), [P, T], F32) for r in range(2)] for half in range(2)]
         sums = [held("sum%d" % half, [P, T], F32) for half in range(2)]
@@ -213,7 +226,7 @@ def tile_moe_duo_gelu_kernel(
 
         def fetch(half, r, t0, t1):
             nc.vector.tensor_tensor(
-                parts[half][r][:, t0:t1], ys[half][:].indirect(places[r][:, t0 // 16 : t1 // 16]), gates[:, r, t0:t1], MULT
+                parts[half][r][:, t0:t1], y[half][:].indirect(places[r][:, t0 // 16 : t1 // 16]), gates[:, r, t0:t1], MULT
             )
 
         def finish(half, t0, t1):
@@ -224,9 +237,7 @@ def tile_moe_duo_gelu_kernel(
         fetch(0, 1, 0, T)
         fetch(1, 0, 0, T)
         finish(0, 0, T)
-        fetch(1, 1, 0, 2 * P)
-        fetch(1, 1, 2 * P, 3 * P)
-        finish(1, 0, 2 * P)
-        fetch(1, 1, 3 * P, T)
-        finish(1, 2 * P, 3 * P)
-        finish(1, 3 * P, T)
+        fetch(1, 1, 0, T // 2)
+        fetch(1, 1, T // 2, T)
+        finish(1, 0, T // 2)
+        finish(1, T // 2, T)

@@ -28,8 +28,8 @@ GROUPS = ((0,), (1, 2), (3, 4), (5, 6), (7,))
 RUNS = ((0, 512), (512, 256), (768, 128), (896, 128))
 
 
-def load_scale_rows(queue, plane, rows, quadrants=range(4)):
-    for q in quadrants:
+def load_scale_rows(queue, plane, rows):
+    for q in range(4):
         queue.dma_start(out=plane[32 * q : 32 * q + 4].bitcast(I32), in_=rows[4 * q : 4 * q + 4])
 
 
@@ -61,13 +61,10 @@ def tile_moe_duo_gelu_kernel(
         w2w = held("w2w", [P, E, 2 * N], U8)
         gates = held("gates", [P, 2, T], F32)
         ident = held("ident", [P, P], F32)
-        warm_in = held("warm_in", [P, 8], F32)
-        warm_out = held("warm_out", [P, 8], F32)
 
         def by_expert(dram):
             return dram.bitcast(I32).rearrange("e o p n -> p (e o) n")
 
-        nc.gpsimd.memset(warm_in[:], 0.0)
         for plane in (w1s, wps):
             nc.vector.memset(plane[:].bitcast(I32), 0)
         nc.vector.memset(ident[:], 0.0)
@@ -92,10 +89,8 @@ def tile_moe_duo_gelu_kernel(
             load_token_scales(nc.scalar, q)
         load_token_scales(nc.sync, 3)
         nc.scalar.dma_start(out=xw[:], in_=x_words.rearrange("o p t d -> p (o t d)").bitcast(I32))
-        nc.scalar.activation(out=warm_out[:], in_=warm_in[:], func=GELU)
         load_scale_rows(nc.sync, w1s, by_expert(w1_scales))
-        load_scale_rows(nc.sync, wps, by_expert(wp_scales), range(1))
-        load_scale_rows(nc.scalar, wps, by_expert(wp_scales), range(1, 4))
+        load_scale_rows(nc.scalar, wps, by_expert(wp_scales))
         for experts in (slice(1, 2), slice(2, 4)):
             load_words(nc.sync, wpw, wp_words, experts)
             load_words(nc.sync, w1w, w1_words, experts)

@@ -91,7 +91,7 @@ def tile_moe_duo_gelu_kernel(
         nc.scalar.dma_start(out=xw[:], in_=x_words.rearrange("o p t d -> p (o t d)").bitcast(I32))
         load_scale_rows(nc.sync, w1s, by_expert(w1_scales))
         load_scale_rows(nc.scalar, wps, by_expert(wp_scales))
-        for experts in (slice(1, 2), slice(2, 4)):
+        for experts in (slice(3, 4), slice(1, 2), slice(2, 3)):
             load_words(nc.sync, wpw, wp_words, experts)
             load_words(nc.sync, w1w, w1_words, experts)
         load_scale_rows(nc.sync, w2s, by_expert(w2_scales))
@@ -99,6 +99,14 @@ def tile_moe_duo_gelu_kernel(
         nc.sync.dma_start(pos1_sb[:], pos1)
         nc.sync.dma_start(pos2_sb[:], pos2)
         nc.sync.dma_start(out=gates[:], in_=gate.rearrange("r p t -> p r t"))
+
+        laid = {}
+        for side, (ww, ws) in ((PARTNER, (wpw, wps)), (TOKEN, (w1w, w1s))):
+            words = held("laid_words%d" % side, [P, 4, P, 2], U8)
+            scales = held("laid_scales%d" % side, [P, 4, P], U8)
+            nc.gpsimd.tensor_copy(out=scales[:], in_=ws[:, E - 1, :].rearrange("p (m t) -> p t m", t=4))
+            nc.gpsimd.tensor_copy(out=words[:], in_=ww[:, E - 1, :].rearrange("p (m t b) -> p t m b", t=4, b=2))
+            laid[side] = (words, scales)
 
         h_turned = [held("h_turned%d" % first, [P, width, 4], BF16) for first, width in RUNS]
 
@@ -135,6 +143,25 @@ def tile_moe_duo_gelu_kernel(
         def first_layer(s0):
             e = s0 // C
             pre = pre_banks.tile([P, H], F32, name="pre")
+            if e == E - 1:
+                for t in range(4):
+                    for side in (PARTNER, TOKEN):
+                        nc.tensor.matmul_mx(
+                            out=pre[:, t * P : (t + 1) * P],
+                            lhsT=laid[side][0][:, t].rearrange("p m b -> p (m b)").bitcast(FP4X4),
+                            lhsT_scale=laid[side][1][:, t, :],
+                            rhs=gathered[side, WORDS, s0].bitcast(FP8X4),
+                            rhs_scale=gathered[side, SCALES, s0],
+                            start=(side == PARTNER),
+                            stop=(side == TOKEN),
+                        )
+                ((first, target),) = [(f, tile) for (f, w), tile in zip(RUNS, h_turned) if f <= s0 < f + w]
+                nc.scalar.activation(
+                    out=target[:, s0 - first : s0 - first + P, :],
+                    in_=pre[:].rearrange("p (t s) -> p s t", t=4),
+                    func=GELU,
+                )
+                return
             for side, (ww, ws) in ((PARTNER, (wpw, wps)), (TOKEN, (w1w, w1s))):
                 nc.tensor.matmul_mx(
                     out=pre[:],
@@ -148,22 +175,17 @@ def tile_moe_duo_gelu_kernel(
             h = ring.tile([P, H], BF16, name="h", align_bytes=64)
             h_view = h[:].rearrange("s (u p d) -> s u p d", u=2, d=2)
             pre_view = pre[:].rearrange("s (p u d) -> s u p d", u=2, d=2)
-            if s0 < LAST:
-                nc.scalar.activation(out=h_view, in_=pre_view, func=GELU)
-            else:
-                for u in range(2):
-                    nc.scalar.activation(out=h_view[:, u], in_=pre_view[:, u], func=GELU)
+            nc.scalar.activation(out=h_view, in_=pre_view, func=GELU)
             hidden[s0] = h
 
         def turn(s0):
             ((first, target),) = [(f, tile) for (f, w), tile in zip(RUNS, h_turned) if f <= s0 < f + w]
-            if s0 < LAST:
-                turned = turn_banks.tile([P, 2, P], F32, name="turn")
-            else:
-                turned = end_banks.tile([P, 2, P], F32, name="last_turn")
+            if s0 >= (E - 1) * C:
+                return
+            turned = turn_banks.tile([P, 2, P], F32, name="turn")
             for u in range(2):
                 nc.tensor.transpose(turned[:, u, :], hidden[s0][:].bitcast(F32)[:, u * P : (u + 1) * P], ident[:])
-            move = nc.vector.tensor_copy if LAST - 2 * P <= s0 < LAST else nc.scalar.copy
+            move = nc.scalar.copy
             move(out=target[:, s0 - first : s0 - first + P, :].bitcast(F32), in_=turned[:].rearrange("p u s -> p s u"))
 
         waiting = []

@@ -22,6 +22,8 @@ ADD = mybir.AluOpType.add
 
 PARTNER, TOKEN = 0, 1
 WORDS, SCALES = 0, 1
+MOVING = 2
+PRE_BANKS = ("pre0", "pre1", "pre0", "pre1", "late0", "late1", "pre1", "turn1")
 LAST = S - P
 
 GROUPS = ((0,), (1, 2), (3, 4), (5, 6), (7,))
@@ -40,9 +42,7 @@ def tile_moe_duo_gelu_kernel(
     with ExitStack() as ctx:
         keep = ctx.enter_context(tc.tile_pool(name="keep", bufs=1))
         ring = ctx.enter_context(tc.tile_pool(name="ring", bufs=4))
-        pre_banks = ctx.enter_context(tc.psum_pool(name="pre_banks", bufs=2))
-        turn_banks = ctx.enter_context(tc.psum_pool(name="turn_banks", bufs=2))
-        end_banks = ctx.enter_context(tc.psum_pool(name="end_banks", bufs=1))
+        banks = ctx.enter_context(tc.psum_pool(name="banks", bufs=1))
 
         def held(name, shape, dtype):
             return keep.tile(shape, dtype, name=name, align_bytes=64)
@@ -53,8 +53,8 @@ def tile_moe_duo_gelu_kernel(
         pos2_sb = held("pos2_sb", [P, T // 16], U16)
         xw = held("xw", [P, T], I32)
         xs = held("xs", [P, T], U8)
-        w1s = held("w1s", [P, E, H], U8)
-        wps = held("wps", [P, E, H], U8)
+        first_scales = held("first_scales", [P, 2, E, H], U8)
+        wps, w1s = first_scales[:, PARTNER], first_scales[:, TOKEN]
         w2s = held("w2s", [P, E, N], U8)
         w1w = held("w1w", [P, E, 2 * H], U8)
         wpw = held("wpw", [P, E, 2 * H], U8)
@@ -66,7 +66,7 @@ def tile_moe_duo_gelu_kernel(
             return dram.bitcast(I32).rearrange("e o p n -> p (e o) n")
 
         for plane in (w1s, wps):
-            nc.vector.memset(plane[:].bitcast(I32), 0)
+            nc.vector.memset(plane.bitcast(I32), 0)
         nc.vector.memset(ident[:], 0.0)
         nc.vector.memset(w2s[:].bitcast(I32), 0)
 
@@ -91,22 +91,24 @@ def tile_moe_duo_gelu_kernel(
         nc.scalar.dma_start(out=xw[:], in_=x_words.rearrange("o p t d -> p (o t d)").bitcast(I32))
         load_scale_rows(nc.sync, w1s, by_expert(w1_scales))
         load_scale_rows(nc.scalar, wps, by_expert(wp_scales))
-        for experts in (slice(3, 4), slice(1, 2), slice(2, 3)):
-            load_words(nc.sync, wpw, wp_words, experts)
-            load_words(nc.sync, w1w, w1_words, experts)
+        for e in (2, 1, 3):
+            load_words(nc.sync, wpw, wp_words, slice(e, e + 1))
+            load_words(nc.sync, w1w, w1_words, slice(e, e + 1))
         load_scale_rows(nc.sync, w2s, by_expert(w2_scales))
         nc.sync.dma_start(out=w2w[:].bitcast(I32), in_=by_expert(w2_words))
         nc.sync.dma_start(pos1_sb[:], pos1)
         nc.sync.dma_start(pos2_sb[:], pos2)
         nc.sync.dma_start(out=gates[:], in_=gate.rearrange("r p t -> p r t"))
 
-        laid = {}
-        for side, (ww, ws) in ((PARTNER, (wpw, wps)), (TOKEN, (w1w, w1s))):
-            words = held("laid_words%d" % side, [P, 4, P, 2], U8)
-            scales = held("laid_scales%d" % side, [P, 4, P], U8)
-            nc.gpsimd.tensor_copy(out=scales[:], in_=ws[:, E - 1, :].rearrange("p (m t) -> p t m", t=4))
-            nc.gpsimd.tensor_copy(out=words[:], in_=ww[:, E - 1, :].rearrange("p (m t b) -> p t m b", t=4, b=2))
-            laid[side] = (words, scales)
+        laid_words, laid_scales = {}, {}
+        for e in range(MOVING, E):
+            laid_scales[e] = held("laid_scales%d" % e, [P, 2, 4, P], U8)
+            nc.gpsimd.tensor_copy(out=laid_scales[e][:], in_=first_scales[:, :, e, :].rearrange("p a (m t) -> p a t m", t=4))
+            for side, ww in ((PARTNER, wpw), (TOKEN, w1w)):
+                laid_words[e, side] = held("laid_words%d_%d" % (e, side), [P, 4, P], U16)
+                nc.gpsimd.tensor_copy(
+                    out=laid_words[e, side][:], in_=ww[:, e, :].bitcast(U16).rearrange("p (m t) -> p t m", t=4)
+                )
 
         h_turned = [held("h_turned%d" % first, [P, width, 4], BF16) for first, width in RUNS]
 
@@ -128,32 +130,26 @@ def tile_moe_duo_gelu_kernel(
                 for side in (PARTNER, TOKEN):
                     gather(side, WORDS, start, width)
 
-        def side_after_side(first, width):
-            for side in (PARTNER, TOKEN):
-                gather(side, WORDS, first, width)
-                gather(side, SCALES, first, width)
-
         scales_then_words(0, P, 2 * P)
-        side_after_side(3 * P, 2 * P)
-        scales_then_words(5 * P, P, P)
-        side_after_side(LAST, P)
+        scales_then_words(3 * P, P, 2 * P)
+        scales_then_words(6 * P, P, P)
 
         hidden = {}
 
         def first_layer(s0):
             e = s0 // C
-            pre = pre_banks.tile([P, H], F32, name="pre")
-            if e == E - 1:
-                for t in range(4):
-                    for side in (PARTNER, TOKEN):
+            pre = banks.tile([P, H], F32, name=PRE_BANKS[s0 // P])
+            if e >= MOVING:
+                for side in (PARTNER, TOKEN):
+                    for t in range(4):
                         nc.tensor.matmul_mx(
                             out=pre[:, t * P : (t + 1) * P],
-                            lhsT=laid[side][0][:, t].rearrange("p m b -> p (m b)").bitcast(FP4X4),
-                            lhsT_scale=laid[side][1][:, t, :],
+                            lhsT=laid_words[e, side][:, t, :].bitcast(FP4X4),
+                            lhsT_scale=laid_scales[e][:, side, t, :],
                             rhs=gathered[side, WORDS, s0].bitcast(FP8X4),
                             rhs_scale=gathered[side, SCALES, s0],
-                            start=(side == PARTNER),
-                            stop=(side == TOKEN),
+                            start=(side == PARTNER and t == 0),
+                            stop=(side == TOKEN and t == 3),
                         )
                 ((first, target),) = [(f, tile) for (f, w), tile in zip(RUNS, h_turned) if f <= s0 < f + w]
                 nc.scalar.activation(
@@ -180,9 +176,9 @@ def tile_moe_duo_gelu_kernel(
 
         def turn(s0):
             ((first, target),) = [(f, tile) for (f, w), tile in zip(RUNS, h_turned) if f <= s0 < f + w]
-            if s0 >= (E - 1) * C:
+            if s0 >= MOVING * C:
                 return
-            turned = turn_banks.tile([P, 2, P], F32, name="turn")
+            turned = banks.tile([P, 2, P], F32, name="turn%d" % (s0 // P % 2))
             for u in range(2):
                 nc.tensor.transpose(turned[:, u, :], hidden[s0][:].bitcast(F32)[:, u * P : (u + 1) * P], ident[:])
             move = nc.scalar.copy
@@ -222,20 +218,20 @@ def tile_moe_duo_gelu_kernel(
                 out=codes[:].bitcast(FP8X4), scales=scales[:], in_=h_turned[r][:].rearrange("p s d -> p (s d)")
             )
             quantised.append((codes, scales, first, width))
-            if width > P:
-                bank = pre_banks.tile([P, width], F32, name="pre")
-            else:
-                bank = end_banks.tile([P, width], F32, name="y_from%d" % first)
-            second_layer(0, bank, 0, *quantised[r])
-            move = nc.scalar.copy if r % 2 else nc.vector.tensor_copy
-            move(out=y[0][:, first : first + width], in_=bank[:])
-        upper = end_banks.tile([P, S // 2], F32, name="last_turn")
-        for codes, scales, first, width in quantised[1:]:
-            second_layer(1, upper, first - S // 2, codes, scales, first, width)
-        nc.scalar.copy(out=y[1][:, S // 2 :], in_=upper[:])
-        lower = end_banks.tile([P, S // 2], F32, name="y_from%d" % LAST)
-        second_layer(1, lower, 0, *quantised[0])
-        nc.scalar.copy(out=y[1][:, : S // 2], in_=lower[:])
+
+        def results(half, name, runs, move):
+            first, end = runs[0][2], runs[-1][2] + runs[-1][3]
+            bank = banks.tile([P, end - first], F32, name=name)
+            for run in runs:
+                second_layer(half, bank, run[2] - first, *run)
+            move(out=y[half][:, first:end], in_=bank[:])
+
+        results(0, PRE_BANKS[6], quantised[:1], nc.scalar.copy)
+        results(0, PRE_BANKS[5], quantised[1:2], nc.scalar.copy)
+        results(0, PRE_BANKS[7], quantised[2:3], nc.vector.tensor_copy)
+        results(0, "last", quantised[3:], nc.scalar.copy)
+        results(1, "last", quantised[:1], nc.scalar.copy)
+        results(1, PRE_BANKS[6], quantised[1:], nc.scalar.copy)
 
         parts = [[held("part%d_%d" % (half, r), [P, T], F32) for r in range(2)] for half in range(2)]
         sums = [held("sum%d" % half, [P, T], F32) for half in range(2)]
@@ -251,9 +247,11 @@ def tile_moe_duo_gelu_kernel(
             nc.sync.dma_start(out=out[P * half : P * (half + 1), t0:t1], in_=sums[half][:, t0:t1])
 
         fetch(0, 0, 0, T)
-        fetch(0, 1, 0, T)
+        fetch(0, 1, 0, T // 2)
+        fetch(0, 1, T // 2, T)
+        finish(0, 0, T // 2)
+        finish(0, T // 2, T)
         fetch(1, 0, 0, T)
-        finish(0, 0, T)
         fetch(1, 1, 0, T // 2)
         fetch(1, 1, T // 2, T)
         finish(1, 0, T // 2)

@@ -17,6 +17,7 @@ U8 = mybir.dt.uint8
 FP8X4 = mybir.dt.float8_e4m3fn_x4
 FP4X4 = mybir.dt.float4_e2m1fn_x4
 GELU = mybir.ActivationFunctionType.Gelu_apprx_tanh
+COPY = mybir.ActivationFunctionType.Copy
 MULT = mybir.AluOpType.mult
 ADD = mybir.AluOpType.add
 
@@ -196,20 +197,6 @@ def tile_moe_duo_gelu_kernel(
 
         y = [held("y%d" % half, [P, S], F32) for half in range(2)]
 
-        def second_layer(half, bank, at, codes, scales, first, width):
-            for c0 in range(0, width, C):
-                cols = slice(c0, min(c0 + C, width))
-                e = (first + c0) // C
-                nc.tensor.matmul_mx(
-                    out=bank[:, at + cols.start : at + cols.stop],
-                    lhsT=w2w[:, e, 2 * P * half : 2 * P * (half + 1)].bitcast(FP4X4),
-                    lhsT_scale=w2s[:, e, P * half : P * (half + 1)],
-                    rhs=codes[:, cols].bitcast(FP8X4),
-                    rhs_scale=scales[:, cols],
-                    start=True,
-                    stop=True,
-                )
-
         quantised = []
         for r, (first, width) in enumerate(RUNS):
             codes = held("hc%d" % first, [P, width], U32)
@@ -219,40 +206,72 @@ def tile_moe_duo_gelu_kernel(
             )
             quantised.append((codes, scales, first, width))
 
-        def results(half, name, runs, move):
-            first, end = runs[0][2], runs[-1][2] + runs[-1][3]
-            bank = banks.tile([P, end - first], F32, name=name)
-            for run in runs:
-                second_layer(half, bank, run[2] - first, *run)
-            move(out=y[half][:, first:end], in_=bank[:])
+        def results(name, pieces, move):
+            bank = banks.tile([P, sum(end - first for half, first, end in pieces)], F32, name=name)
+            at = 0
+            for half, first, end in pieces:
+                for codes, scales, q0, width in quantised:
+                    lo, hi = max(first, q0), min(end, q0 + width)
+                    for c0 in range(lo, hi, P):
+                        if c0 > lo and c0 % C:
+                            continue
+                        c1 = min(hi, (c0 // C + 1) * C)
+                        nc.tensor.matmul_mx(
+                            out=bank[:, at + c0 - first : at + c1 - first],
+                            lhsT=w2w[:, c0 // C, 2 * P * half : 2 * P * (half + 1)].bitcast(FP4X4),
+                            lhsT_scale=w2s[:, c0 // C, P * half : P * (half + 1)],
+                            rhs=codes[:, c0 - q0 : c1 - q0].bitcast(FP8X4),
+                            rhs_scale=scales[:, c0 - q0 : c1 - q0],
+                            start=True,
+                            stop=True,
+                        )
+                at = at + end - first
+            at = 0
+            for half, first, end in pieces:
+                move(out=y[half][:, first:end], in_=bank[:, at : at + end - first])
+                at = at + end - first
 
-        results(0, PRE_BANKS[6], quantised[:1], nc.scalar.copy)
-        results(0, PRE_BANKS[5], quantised[1:2], nc.scalar.copy)
-        results(0, PRE_BANKS[7], quantised[2:3], nc.vector.tensor_copy)
-        results(0, "last", quantised[3:], nc.scalar.copy)
-        results(1, "last", quantised[:1], nc.scalar.copy)
-        results(1, PRE_BANKS[6], quantised[1:], nc.scalar.copy)
+        results(PRE_BANKS[6], [(0, 0, 512)], nc.scalar.copy)
+        results(PRE_BANKS[5], [(0, 512, 768)], nc.scalar.copy)
+        results(PRE_BANKS[7], [(0, 768, 896), (1, 0, 256)], nc.vector.tensor_copy)
+        results("last", [(0, 896, 1024)], nc.scalar.copy)
+        results(PRE_BANKS[4], [(1, 256, 768)], nc.scalar.copy)
+        results("turn0", [(1, 768, 1024)], nc.scalar.copy)
 
         parts = [[held("part%d_%d" % (half, r), [P, T], F32) for r in range(2)] for half in range(2)]
+        picked = [[held("picked%d_%d" % (half, r), [P, T], F32) for r in range(2)] for half in range(2)]
         sums = [held("sum%d" % half, [P, T], F32) for half in range(2)]
         places = (pos1_sb, pos2_sb)
 
+        def window(half, r, t0, t1):
+            return y[half][:].indirect(places[r][:, t0 // 16 : t1 // 16])
+
         def fetch(half, r, t0, t1):
-            nc.vector.tensor_tensor(
-                parts[half][r][:, t0:t1], y[half][:].indirect(places[r][:, t0 // 16 : t1 // 16]), gates[:, r, t0:t1], MULT
-            )
+            nc.vector.tensor_tensor(parts[half][r][:, t0:t1], window(half, r, t0, t1), gates[:, r, t0:t1], MULT)
+
+        def pick(half, r, t0, t1):
+            nc.scalar.activation(out=picked[half][r][:, t0:t1], in_=window(half, r, t0, t1), func=COPY)
+
+        def weigh(half, r, t0, t1):
+            nc.vector.tensor_tensor(parts[half][r][:, t0:t1], picked[half][r][:, t0:t1], gates[:, r, t0:t1], MULT)
 
         def finish(half, t0, t1):
             nc.vector.tensor_tensor(sums[half][:, t0:t1], parts[half][0][:, t0:t1], parts[half][1][:, t0:t1], ADD)
             nc.sync.dma_start(out=out[P * half : P * (half + 1), t0:t1], in_=sums[half][:, t0:t1])
 
+        pick(0, 1, 256, 512)
+        pick(1, 0, 0, 512)
+        pick(1, 1, 0, 256)
+        pick(1, 1, 256, 384)
         fetch(0, 0, 0, T)
-        fetch(0, 1, 0, T // 2)
-        fetch(0, 1, T // 2, T)
-        finish(0, 0, T // 2)
-        finish(0, T // 2, T)
-        fetch(1, 0, 0, T)
-        fetch(1, 1, 0, T // 2)
-        fetch(1, 1, T // 2, T)
-        finish(1, 0, T // 2)
-        finish(1, T // 2, T)
+        fetch(0, 1, 0, 256)
+        weigh(0, 1, 256, 512)
+        finish(0, 0, 256)
+        finish(0, 256, 512)
+        fetch(1, 1, 384, 512)
+        weigh(1, 0, 0, 512)
+        weigh(1, 1, 0, 256)
+        finish(1, 384, 512)
+        finish(1, 0, 256)
+        weigh(1, 1, 256, 384)
+        finish(1, 256, 384)

@@ -100,6 +100,10 @@ def tile_moe_duo_gelu_kernel(
         nc.sync.dma_start(pos1_sb[:], pos1)
         nc.sync.dma_start(pos2_sb[:], pos2)
         nc.sync.dma_start(out=gates[:], in_=gate.rearrange("r p t -> p r t"))
+        gate_columns = [held("gate_columns%d" % r, [P, T // P], F32) for r in range(2)]
+        with nc.allow_non_contiguous_dma(reason="one gate value a partition"):
+            for r in range(2):
+                nc.sync.dma_start(out=gate_columns[r][:], in_=gate[r, 0, :].rearrange("(c t) -> t c", t=P))
 
         laid_words, laid_scales = {}, {}
         for e in range(MOVING, E):
@@ -195,7 +199,7 @@ def tile_moe_duo_gelu_kernel(
             waiting = waiting[-1:]
         turn(LAST)
 
-        y = [held("y%d" % half, [P, S], F32) for half in range(2)]
+        y = [held(name, [P, S], F32) for name in ("y0", "h_turned%d" % LAST)]
 
         quantised = []
         for r, (first, width) in enumerate(RUNS):
@@ -231,47 +235,57 @@ def tile_moe_duo_gelu_kernel(
                 move(out=y[half][:, first:end], in_=bank[:, at : at + end - first])
                 at = at + end - first
 
-        results(PRE_BANKS[6], [(0, 0, 512)], nc.scalar.copy)
-        results(PRE_BANKS[5], [(0, 512, 768)], nc.scalar.copy)
-        results(PRE_BANKS[7], [(0, 768, 896), (1, 0, 256)], nc.vector.tensor_copy)
+        results(PRE_BANKS[4], [(0, 0, 256)], nc.vector.tensor_copy)
+        results(PRE_BANKS[5], [(0, 256, 768)], nc.scalar.copy)
+        results(PRE_BANKS[6], [(0, 768, 896)], nc.scalar.copy)
         results("last", [(0, 896, 1024)], nc.scalar.copy)
-        results(PRE_BANKS[4], [(1, 256, 768)], nc.scalar.copy)
-        results("turn0", [(1, 768, 1024)], nc.scalar.copy)
+        results("turn0", [(1, 0, 512)], nc.vector.tensor_copy)
+        results(PRE_BANKS[7], [(1, 512, 1024)], nc.scalar.copy)
 
-        parts = [[held("part%d_%d" % (half, r), [P, T], F32) for r in range(2)] for half in range(2)]
-        picked = [[held("picked%d_%d" % (half, r), [P, T], F32) for r in range(2)] for half in range(2)]
-        sums = [held("sum%d" % half, [P, T], F32) for half in range(2)]
         places = (pos1_sb, pos2_sb)
 
         def window(half, r, t0, t1):
             return y[half][:].indirect(places[r][:, t0 // 16 : t1 // 16])
 
-        def fetch(half, r, t0, t1):
-            nc.vector.tensor_tensor(parts[half][r][:, t0:t1], window(half, r, t0, t1), gates[:, r, t0:t1], MULT)
+        gate_banks = []
+        for b, name in enumerate((PRE_BANKS[5], "last")):
+            bank = banks.tile([P, 2, C], F32, name=name)
+            for r in range(2):
+                for c in range(2):
+                    column = gate_columns[r][:, 2 * b + c : 2 * b + c + 1]
+                    nc.tensor.transpose(bank[:, r, c * P : (c + 1) * P], column.to_broadcast([P, P]), ident[:])
+            gate_banks.append(bank)
 
-        def pick(half, r, t0, t1):
-            nc.scalar.activation(out=picked[half][r][:, t0:t1], in_=window(half, r, t0, t1), func=COPY)
+        def finish(engine, half, t0, t1, first, second):
+            total = held("sum%d_%d" % (half, t0), [P, t1 - t0], F32)
+            engine.tensor_tensor(total[:], first, second, ADD)
+            nc.sync.dma_start(out=out[P * half : P * (half + 1), t0:t1], in_=total[:])
 
-        def weigh(half, r, t0, t1):
-            nc.vector.tensor_tensor(parts[half][r][:, t0:t1], picked[half][r][:, t0:t1], gates[:, r, t0:t1], MULT)
+        ranges = ((0, 256), (256, 448), (448, 512))
+        picked, weighed = {}, {}
+        for t0, t1 in ranges:
+            picked[t0] = held("picked%d" % t0, [P, 2, t1 - t0], F32)
+            for r in range(2):
+                nc.scalar.activation(out=picked[t0][:, r, :], in_=window(1, r, t0, t1), func=COPY)
 
-        def finish(half, t0, t1):
-            nc.vector.tensor_tensor(sums[half][:, t0:t1], parts[half][0][:, t0:t1], parts[half][1][:, t0:t1], ADD)
-            nc.sync.dma_start(out=out[P * half : P * (half + 1), t0:t1], in_=sums[half][:, t0:t1])
+        first_part = held("first_part", [P, T], F32)
+        nc.vector.tensor_tensor(first_part[:], window(0, 0, 0, T), gates[:, 0, :], MULT)
+        for t0 in (0, C):
+            second_part = held("second_part%d" % t0, [P, C], F32)
+            nc.vector.tensor_tensor(second_part[:], window(0, 1, t0, t0 + C), gates[:, 1, t0 : t0 + C], MULT)
+            finish(nc.gpsimd, 0, t0, t0 + C, first_part[:, t0 : t0 + C], second_part[:])
 
-        pick(0, 1, 256, 512)
-        pick(1, 0, 0, 512)
-        pick(1, 1, 0, 256)
-        pick(1, 1, 256, 384)
-        fetch(0, 0, 0, T)
-        fetch(0, 1, 0, 256)
-        weigh(0, 1, 256, 512)
-        finish(0, 0, 256)
-        finish(0, 256, 512)
-        fetch(1, 1, 384, 512)
-        weigh(1, 0, 0, 512)
-        weigh(1, 1, 0, 256)
-        finish(1, 384, 512)
-        finish(1, 0, 256)
-        weigh(1, 1, 256, 384)
-        finish(1, 256, 384)
+        def weigh(t0, t1):
+            weighed[t0] = held("weighed%d" % t0, [P, 2, t1 - t0], F32)
+            bank = gate_banks[t0 // C]
+            nc.vector.tensor_tensor(weighed[t0][:], picked[t0][:], bank[:, :, t0 % C : t0 % C + t1 - t0], MULT)
+
+        def add(t0, t1):
+            finish(nc.vector, 1, t0, t1, weighed[t0][:, 0, :], weighed[t0][:, 1, :])
+
+        weigh(*ranges[0])
+        weigh(*ranges[1])
+        add(*ranges[0])
+        weigh(*ranges[2])
+        add(*ranges[1])
+        add(*ranges[2])

@@ -100,10 +100,6 @@ def tile_moe_duo_gelu_kernel(
         nc.sync.dma_start(pos1_sb[:], pos1)
         nc.sync.dma_start(pos2_sb[:], pos2)
         nc.sync.dma_start(out=gates[:], in_=gate.rearrange("r p t -> p r t"))
-        gate_columns = [held("gate_columns%d" % r, [P, T // P], F32) for r in range(2)]
-        with nc.allow_non_contiguous_dma(reason="one gate value a partition"):
-            for r in range(2):
-                nc.sync.dma_start(out=gate_columns[r][:], in_=gate[r, 0, :].rearrange("(c t) -> t c", t=P))
 
         laid_words, laid_scales = {}, {}
         for e in range(MOVING, E):
@@ -135,8 +131,12 @@ def tile_moe_duo_gelu_kernel(
                 for side in (PARTNER, TOKEN):
                     gather(side, WORDS, start, width)
 
-        scales_then_words(0, P, 2 * P)
-        scales_then_words(3 * P, P, 2 * P)
+        for first in (0, 3 * P):
+            for side in (PARTNER, TOKEN):
+                gather(side, SCALES, first, 3 * P)
+            gather(PARTNER, WORDS, first, 3 * P)
+            gather(TOKEN, WORDS, first, P)
+            gather(TOKEN, WORDS, first + P, 2 * P)
         scales_then_words(6 * P, P, P)
 
         hidden = {}
@@ -247,20 +247,14 @@ def tile_moe_duo_gelu_kernel(
         def window(half, r, t0, t1):
             return y[half][:].indirect(places[r][:, t0 // 16 : t1 // 16])
 
-        gate_banks = []
-        for b, name in enumerate((PRE_BANKS[5], "last")):
-            bank = banks.tile([P, 2, C], F32, name=name)
-            for r in range(2):
-                for c in range(2):
-                    column = gate_columns[r][:, 2 * b + c : 2 * b + c + 1]
-                    nc.tensor.transpose(bank[:, r, c * P : (c + 1) * P], column.to_broadcast([P, P]), ident[:])
-            gate_banks.append(bank)
-
-        def finish(engine, half, t0, t1, first, second):
+        def finish(half, t0, t1, first, second):
             total = held("sum%d_%d" % (half, t0), [P, t1 - t0], F32)
-            engine.tensor_tensor(total[:], first, second, ADD)
+            nc.vector.tensor_tensor(total[:], first, second, ADD)
             nc.sync.dma_start(out=out[P * half : P * (half + 1), t0:t1], in_=total[:])
 
+        split = 320
+        rest = held("rest", [P, T - split], F32)
+        nc.scalar.activation(out=rest[:], in_=window(0, 1, split, T), func=COPY)
         ranges = ((0, 256), (256, 448), (448, 512))
         picked, weighed = {}, {}
         for t0, t1 in ranges:
@@ -269,19 +263,19 @@ def tile_moe_duo_gelu_kernel(
                 nc.scalar.activation(out=picked[t0][:, r, :], in_=window(1, r, t0, t1), func=COPY)
 
         first_part = held("first_part", [P, T], F32)
+        second_part = held("second_part", [P, T], F32)
         nc.vector.tensor_tensor(first_part[:], window(0, 0, 0, T), gates[:, 0, :], MULT)
-        for t0 in (0, C):
-            second_part = held("second_part%d" % t0, [P, C], F32)
-            nc.vector.tensor_tensor(second_part[:], window(0, 1, t0, t0 + C), gates[:, 1, t0 : t0 + C], MULT)
-            finish(nc.gpsimd, 0, t0, t0 + C, first_part[:, t0 : t0 + C], second_part[:])
+        nc.vector.tensor_tensor(second_part[:, :split], window(0, 1, 0, split), gates[:, 1, :split], MULT)
+        nc.vector.tensor_tensor(second_part[:, split:], rest[:], gates[:, 1, split:], MULT)
+        finish(0, 0, split, first_part[:, :split], second_part[:, :split])
+        finish(0, split, T, first_part[:, split:], second_part[:, split:])
 
         def weigh(t0, t1):
             weighed[t0] = held("weighed%d" % t0, [P, 2, t1 - t0], F32)
-            bank = gate_banks[t0 // C]
-            nc.vector.tensor_tensor(weighed[t0][:], picked[t0][:], bank[:, :, t0 % C : t0 % C + t1 - t0], MULT)
+            nc.vector.tensor_tensor(weighed[t0][:], picked[t0][:], gates[:, :, t0:t1], MULT)
 
         def add(t0, t1):
-            finish(nc.vector, 1, t0, t1, weighed[t0][:, 0, :], weighed[t0][:, 1, :])
+            finish(1, t0, t1, weighed[t0][:, 0, :], weighed[t0][:, 1, :])
 
         weigh(*ranges[0])
         weigh(*ranges[1])

@@ -68,14 +68,13 @@ def tile_moe_duo_gelu_kernel(
 
         for plane in (w1s, wps):
             nc.vector.memset(plane.bitcast(I32), 0)
-        nc.vector.memset(ident[:], 0.0)
-        nc.vector.memset(w2s[:].bitcast(I32), 0)
 
         def load_words(queue, tile, dram, experts):
             queue.dma_start(out=tile[:, experts, :].bitcast(I32), in_=by_expert(dram)[:, experts, :])
 
         load_words(nc.gpsimd, wpw, wp_words, slice(0, 1))
-        make_identity(nc, ident[:], nomemset=True)
+        make_identity(nc, ident[:])
+        nc.gpsimd.memset(w2s[:].bitcast(I32), 0)
 
         x_rows = x_scales.bitcast(I32).rearrange("o b t -> b (o t)")
 

@@ -99,6 +99,10 @@ def tile_moe_duo_gelu_kernel(
         nc.sync.dma_start(pos1_sb[:], pos1)
         nc.sync.dma_start(pos2_sb[:], pos2)
         nc.sync.dma_start(out=gates[:], in_=gate.rearrange("r p t -> p r t"))
+        gate_columns = [held("gate_columns%d" % r, [P, T // P], F32) for r in range(2)]
+        with nc.allow_non_contiguous_dma(reason="one gate value a partition"):
+            for r in range(2):
+                nc.sync.dma_start(out=gate_columns[r][:], in_=gate[r, 0, :].rearrange("(c t) -> t c", t=P))
 
         laid_words, laid_scales = {}, {}
         for e in range(MOVING, E):
@@ -246,14 +250,20 @@ def tile_moe_duo_gelu_kernel(
         def window(half, r, t0, t1):
             return y[half][:].indirect(places[r][:, t0 // 16 : t1 // 16])
 
-        def finish(half, t0, t1, first, second):
+        gate_banks = []
+        for b, name in enumerate((PRE_BANKS[5], "last")):
+            bank = banks.tile([P, 2, C], F32, name=name)
+            for r in range(2):
+                for c in range(2):
+                    column = gate_columns[r][:, 2 * b + c : 2 * b + c + 1]
+                    nc.tensor.transpose(bank[:, r, c * P : (c + 1) * P], column.to_broadcast([P, P]), ident[:])
+            gate_banks.append(bank)
+
+        def finish(engine, half, t0, t1, first, second):
             total = held("sum%d_%d" % (half, t0), [P, t1 - t0], F32)
-            nc.vector.tensor_tensor(total[:], first, second, ADD)
+            engine.tensor_tensor(total[:], first, second, ADD)
             nc.sync.dma_start(out=out[P * half : P * (half + 1), t0:t1], in_=total[:])
 
-        split = 320
-        rest = held("rest", [P, T - split], F32)
-        nc.scalar.activation(out=rest[:], in_=window(0, 1, split, T), func=COPY)
         ranges = ((0, 256), (256, 448), (448, 512))
         picked, weighed = {}, {}
         for t0, t1 in ranges:
@@ -262,19 +272,22 @@ def tile_moe_duo_gelu_kernel(
                 nc.scalar.activation(out=picked[t0][:, r, :], in_=window(1, r, t0, t1), func=COPY)
 
         first_part = held("first_part", [P, T], F32)
-        second_part = held("second_part", [P, T], F32)
         nc.vector.tensor_tensor(first_part[:], window(0, 0, 0, T), gates[:, 0, :], MULT)
-        nc.vector.tensor_tensor(second_part[:, :split], window(0, 1, 0, split), gates[:, 1, :split], MULT)
-        nc.vector.tensor_tensor(second_part[:, split:], rest[:], gates[:, 1, split:], MULT)
-        finish(0, 0, split, first_part[:, :split], second_part[:, :split])
-        finish(0, split, T, first_part[:, split:], second_part[:, split:])
+        split = 320
+        second_parts = {}
+        for t0, t1 in ((split, T), (0, split)):
+            second_parts[t0] = held("second_part%d" % t0, [P, t1 - t0], F32)
+            nc.vector.tensor_tensor(second_parts[t0][:], window(0, 1, t0, t1), gates[:, 1, t0:t1], MULT)
+        finish(nc.vector, 0, split, T, first_part[:, split:], second_parts[split][:])
+        finish(nc.gpsimd, 0, 0, split, first_part[:, :split], second_parts[0][:])
 
         def weigh(t0, t1):
             weighed[t0] = held("weighed%d" % t0, [P, 2, t1 - t0], F32)
-            nc.vector.tensor_tensor(weighed[t0][:], picked[t0][:], gates[:, :, t0:t1], MULT)
+            bank = gate_banks[t0 // C]
+            nc.vector.tensor_tensor(weighed[t0][:], picked[t0][:], bank[:, :, t0 % C : t0 % C + t1 - t0], MULT)
 
         def add(t0, t1):
-            finish(1, t0, t1, weighed[t0][:, 0, :], weighed[t0][:, 1, :])
+            finish(nc.vector, 1, t0, t1, weighed[t0][:, 0, :], weighed[t0][:, 1, :])
 
         weigh(*ranges[0])
         weigh(*ranges[1])

@@ -72,7 +72,6 @@ def tile_moe_duo_gelu_kernel(
         def load_words(queue, tile, dram, experts):
             queue.dma_start(out=tile[:, experts, :].bitcast(I32), in_=by_expert(dram)[:, experts, :])
 
-        load_words(nc.gpsimd, wpw, wp_words, slice(0, 1))
         make_identity(nc, ident[:])
         nc.gpsimd.memset(w2s[:].bitcast(I32), 0)
 
@@ -82,7 +81,7 @@ def tile_moe_duo_gelu_kernel(
             rows = x_rows[4 * q : 4 * q + 4].unsqueeze(0).broadcast_to([8, 4, T // 4])
             queue.dma_start(out=xs[32 * q : 32 * q + 32].bitcast(I32), in_=rows)
 
-        load_words(nc.sync, w1w, w1_words, slice(0, 1))
+        load_words(nc.sync, wpw, wp_words, slice(0, 1))
         nc.sync.dma_start(offs2_sb[:], offs2)
         nc.sync.dma_start(offs_sb[:], offs)
         for q in range(3):
@@ -90,6 +89,7 @@ def tile_moe_duo_gelu_kernel(
         load_token_scales(nc.sync, 3)
         nc.scalar.dma_start(out=xw[:], in_=x_words.rearrange("o p t d -> p (o t d)").bitcast(I32))
         load_scale_rows(nc.sync, w1s, by_expert(w1_scales))
+        load_words(nc.sync, w1w, w1_words, slice(0, 1))
         load_scale_rows(nc.scalar, wps, by_expert(wp_scales))
         for e in (2, 1, 3):
             load_words(nc.sync, wpw, wp_words, slice(e, e + 1))
@@ -138,8 +138,11 @@ def tile_moe_duo_gelu_kernel(
             for side in (PARTNER, TOKEN):
                 gather(side, SCALES, first, 3 * P)
             gather(PARTNER, WORDS, first, 3 * P)
-            gather(TOKEN, WORDS, first, P)
-            gather(TOKEN, WORDS, first + P, 2 * P)
+            if first:
+                gather(TOKEN, WORDS, first, P)
+                gather(TOKEN, WORDS, first + P, 2 * P)
+            else:
+                gather(TOKEN, WORDS, first, 3 * P)
         scales_then_words(6 * P, P, P)
 
         hidden = {}
@@ -243,7 +246,8 @@ def tile_moe_duo_gelu_kernel(
         results(PRE_BANKS[6], [(0, 768, 896)], nc.scalar.copy)
         results("last", [(0, 896, 1024)], nc.scalar.copy)
         results("turn0", [(1, 0, 512)], nc.vector.tensor_copy)
-        results(PRE_BANKS[7], [(1, 512, 1024)], nc.scalar.copy)
+        results("pre0", [(1, 512, 768)], nc.scalar.copy)
+        results(PRE_BANKS[7], [(1, 768, 1024)], nc.scalar.copy)
 
         places = (pos1_sb, pos2_sb)
 
@@ -264,22 +268,25 @@ def tile_moe_duo_gelu_kernel(
             engine.tensor_tensor(total[:], first, second, ADD)
             nc.sync.dma_start(out=out[P * half : P * (half + 1), t0:t1], in_=total[:])
 
-        ranges = ((0, 256), (256, 448), (448, 512))
+        ranges = ((0, 256), (256, 384), (384, 512))
+        split = 352
         picked, weighed = {}, {}
-        for t0, t1 in ranges:
+
+        def pick(t0, t1):
             picked[t0] = held("picked%d" % t0, [P, 2, t1 - t0], F32)
             for r in range(2):
                 nc.scalar.activation(out=picked[t0][:, r, :], in_=window(1, r, t0, t1), func=COPY)
 
+        rest = held("rest", [P, T - split], F32)
+        nc.scalar.activation(out=rest[:], in_=window(0, 1, split, T), func=COPY)
+        for piece in ranges:
+            pick(*piece)
+
         first_part = held("first_part", [P, T], F32)
         nc.vector.tensor_tensor(first_part[:], window(0, 0, 0, T), gates[:, 0, :], MULT)
-        split = 320
-        second_parts = {}
-        for t0, t1 in ((split, T), (0, split)):
-            second_parts[t0] = held("second_part%d" % t0, [P, t1 - t0], F32)
-            nc.vector.tensor_tensor(second_parts[t0][:], window(0, 1, t0, t1), gates[:, 1, t0:t1], MULT)
-        finish(nc.vector, 0, split, T, first_part[:, split:], second_parts[split][:])
-        finish(nc.gpsimd, 0, 0, split, first_part[:, :split], second_parts[0][:])
+        second_part = held("second_part", [P, split], F32)
+        nc.vector.tensor_tensor(second_part[:], window(0, 1, 0, split), gates[:, 1, :split], MULT)
+        finish(nc.gpsimd, 0, 0, split, first_part[:, :split], second_part[:])
 
         def weigh(t0, t1):
             weighed[t0] = held("weighed%d" % t0, [P, 2, t1 - t0], F32)
@@ -289,9 +296,12 @@ def tile_moe_duo_gelu_kernel(
         def add(t0, t1):
             finish(nc.vector, 1, t0, t1, weighed[t0][:, 0, :], weighed[t0][:, 1, :])
 
+        rest_weighed = held("rest_weighed", [P, T - split], F32)
+        nc.vector.tensor_tensor(rest_weighed[:], rest[:], gate_banks[1][:, 1, split - C :], MULT)
         weigh(*ranges[0])
         weigh(*ranges[1])
         add(*ranges[0])
         weigh(*ranges[2])
+        finish(nc.vector, 0, split, T, first_part[:, split:], rest_weighed[:])
         add(*ranges[1])
         add(*ranges[2])

@@ -270,6 +270,7 @@ def tile_moe_duo_gelu_kernel(
 
         ranges = ((0, 256), (256, 384), (384, 512))
         split = 352
+        share = 288
         picked, weighed = {}, {}
 
         def pick(t0, t1):
@@ -284,9 +285,9 @@ def tile_moe_duo_gelu_kernel(
 
         first_part = held("first_part", [P, T], F32)
         nc.vector.tensor_tensor(first_part[:], window(0, 0, 0, T), gates[:, 0, :], MULT)
-        second_part = held("second_part", [P, split], F32)
-        nc.vector.tensor_tensor(second_part[:], window(0, 1, 0, split), gates[:, 1, :split], MULT)
-        finish(nc.gpsimd, 0, 0, split, first_part[:, :split], second_part[:])
+        second_part = held("second_part", [P, T], F32)
+        nc.vector.tensor_tensor(second_part[:, :split], window(0, 1, 0, split), gates[:, 1, :split], MULT)
+        finish(nc.gpsimd, 0, 0, share, first_part[:, :share], second_part[:, :share])
 
         def weigh(t0, t1):
             weighed[t0] = held("weighed%d" % t0, [P, 2, t1 - t0], F32)
@@ -296,12 +297,11 @@ def tile_moe_duo_gelu_kernel(
         def add(t0, t1):
             finish(nc.vector, 1, t0, t1, weighed[t0][:, 0, :], weighed[t0][:, 1, :])
 
-        rest_weighed = held("rest_weighed", [P, T - split], F32)
-        nc.vector.tensor_tensor(rest_weighed[:], rest[:], gate_banks[1][:, 1, split - C :], MULT)
+        nc.vector.tensor_tensor(second_part[:, split:], rest[:], gate_banks[1][:, 1, split - C :], MULT)
         weigh(*ranges[0])
         weigh(*ranges[1])
         add(*ranges[0])
         weigh(*ranges[2])
-        finish(nc.vector, 0, split, T, first_part[:, split:], rest_weighed[:])
+        finish(nc.vector, 0, share, T, first_part[:, share:], second_part[:, share:])
         add(*ranges[1])
         add(*ranges[2])

@@ -25,6 +25,7 @@ PARTNER, TOKEN = 0, 1
 WORDS, SCALES = 0, 1
 MOVING = 2
 PRE_BANKS = ("pre0", "pre1", "pre0", "pre1", "late0", "late1", "pre1", "turn1")
+SPLIT = 352
 LAST = S - P
 
 GROUPS = ((0,), (1, 2), (3, 4), (5, 6), (7,))
@@ -60,7 +61,7 @@ def tile_moe_duo_gelu_kernel(
         w1w = held("w1w", [P, E, 2 * H], U8)
         wpw = held("wpw", [P, E, 2 * H], U8)
         w2w = held("w2w", [P, E, 2 * N], U8)
-        gates = held("gates", [P, 2, T], F32)
+        gates = [held("gates%d" % r, [P, width], F32) for r, width in enumerate((T, SPLIT))]
         ident = held("ident", [P, P], F32)
 
         def by_expert(dram):
@@ -98,7 +99,8 @@ def tile_moe_duo_gelu_kernel(
         nc.sync.dma_start(out=w2w[:].bitcast(I32), in_=by_expert(w2_words))
         nc.sync.dma_start(pos1_sb[:], pos1)
         nc.sync.dma_start(pos2_sb[:], pos2)
-        nc.sync.dma_start(out=gates[:], in_=gate.rearrange("r p t -> p r t"))
+        for r, width in enumerate((T, SPLIT)):
+            nc.sync.dma_start(out=gates[r][:], in_=gate[r, :, :width])
         gate_columns = [held("gate_columns%d" % r, [P, T // P], F32) for r in range(2)]
         with nc.allow_non_contiguous_dma(reason="one gate value a partition"):
             for r in range(2):
@@ -269,7 +271,7 @@ def tile_moe_duo_gelu_kernel(
             nc.sync.dma_start(out=out[P * half : P * (half + 1), t0:t1], in_=total[:])
 
         ranges = ((0, 256), (256, 384), (384, 512))
-        split = 352
+        split = SPLIT
         share = 288
         picked, weighed = {}, {}
 
@@ -284,9 +286,9 @@ def tile_moe_duo_gelu_kernel(
             pick(*piece)
 
         first_part = held("first_part", [P, T], F32)
-        nc.vector.tensor_tensor(first_part[:], window(0, 0, 0, T), gates[:, 0, :], MULT)
+        nc.vector.tensor_tensor(first_part[:], window(0, 0, 0, T), gates[0][:], MULT)
         second_part = held("second_part", [P, T], F32)
-        nc.vector.tensor_tensor(second_part[:, :split], window(0, 1, 0, split), gates[:, 1, :split], MULT)
+        nc.vector.tensor_tensor(second_part[:, :split], window(0, 1, 0, split), gates[1][:], MULT)
         finish(nc.gpsimd, 0, 0, share, first_part[:, :share], second_part[:, :share])
 
         def weigh(t0, t1):

@@ -82,12 +82,13 @@ def tile_moe_duo_gelu_kernel(
             rows = x_rows[4 * q : 4 * q + 4].unsqueeze(0).broadcast_to([8, 4, T // 4])
             queue.dma_start(out=xs[32 * q : 32 * q + 32].bitcast(I32), in_=rows)
 
-        load_words(nc.sync, wpw, wp_words, slice(0, 1))
         nc.sync.dma_start(offs2_sb[:], offs2)
+        load_token_scales(nc.sync, 0)
         nc.sync.dma_start(offs_sb[:], offs)
-        for q in range(3):
+        load_token_scales(nc.sync, 1)
+        for q in (2, 3):
             load_token_scales(nc.scalar, q)
-        load_token_scales(nc.sync, 3)
+        load_words(nc.scalar, wpw, wp_words, slice(0, 1))
         nc.scalar.dma_start(out=xw[:], in_=x_words.rearrange("o p t d -> p (o t d)").bitcast(I32))
         load_scale_rows(nc.sync, w1s, by_expert(w1_scales))
         load_words(nc.sync, w1w, w1_words, slice(0, 1))

@@ -32,8 +32,8 @@ GROUPS = ((0,), (1, 2), (3, 4), (5, 6), (7,))
 RUNS = ((0, 512), (512, 256), (768, 128), (896, 128))
 
 
-def load_scale_rows(queue, plane, rows):
-    for q in range(4):
+def load_scale_rows(queue, plane, rows, quadrants):
+    for q in quadrants:
         queue.dma_start(out=plane[32 * q : 32 * q + 4].bitcast(I32), in_=rows[4 * q : 4 * q + 4])
 
 
@@ -67,7 +67,7 @@ def tile_moe_duo_gelu_kernel(
         def by_expert(dram):
             return dram.bitcast(I32).rearrange("e o p n -> p (e o) n")
 
-        for plane in (w1s, wps):
+        for plane in (wps, w1s):
             nc.vector.memset(plane.bitcast(I32), 0)
 
         def load_words(queue, tile, dram, experts):
@@ -88,15 +88,16 @@ def tile_moe_duo_gelu_kernel(
         load_token_scales(nc.sync, 1)
         for q in (2, 3):
             load_token_scales(nc.scalar, q)
-        load_words(nc.scalar, wpw, wp_words, slice(0, 1))
+        load_scale_rows(nc.scalar, wps, by_expert(wp_scales), range(1))
         nc.scalar.dma_start(out=xw[:], in_=x_words.rearrange("o p t d -> p (o t d)").bitcast(I32))
-        load_scale_rows(nc.sync, w1s, by_expert(w1_scales))
+        load_words(nc.sync, wpw, wp_words, slice(0, 1))
+        load_scale_rows(nc.sync, wps, by_expert(wp_scales), range(1, 4))
         load_words(nc.sync, w1w, w1_words, slice(0, 1))
-        load_scale_rows(nc.scalar, wps, by_expert(wp_scales))
+        load_scale_rows(nc.scalar, w1s, by_expert(w1_scales), range(4))
         for e in (2, 1, 3):
             load_words(nc.sync, wpw, wp_words, slice(e, e + 1))
             load_words(nc.sync, w1w, w1_words, slice(e, e + 1))
-        load_scale_rows(nc.sync, w2s, by_expert(w2_scales))
+        load_scale_rows(nc.sync, w2s, by_expert(w2_scales), range(4))
         nc.sync.dma_start(out=w2w[:].bitcast(I32), in_=by_expert(w2_words))
         nc.sync.dma_start(pos1_sb[:], pos1)
         nc.sync.dma_start(pos2_sb[:], pos2)

@@ -304,8 +304,8 @@ def tile_moe_duo_gelu_kernel(
         nc.vector.tensor_tensor(second_part[:, split:], rest[:], gate_banks[1][:, 1, split - C :], MULT)
         weigh(*ranges[0])
         weigh(*ranges[1])
+        finish(nc.vector, 0, share, T, first_part[:, share:], second_part[:, share:])
         add(*ranges[0])
         weigh(*ranges[2])
-        finish(nc.vector, 0, share, T, first_part[:, share:], second_part[:, share:])
         add(*ranges[1])
         add(*ranges[2])

@@ -139,9 +139,12 @@ def tile_moe_duo_gelu_kernel(
                     gather(side, WORDS, start, width)
 
         for first in (0, 3 * P):
-            for side in (PARTNER, TOKEN):
-                gather(side, SCALES, first, 3 * P)
-            gather(PARTNER, WORDS, first, 3 * P)
+            for side, sort in (
+                ((PARTNER, SCALES), (PARTNER, WORDS), (TOKEN, SCALES))
+                if first
+                else ((PARTNER, SCALES), (TOKEN, SCALES), (PARTNER, WORDS))
+            ):
+                gather(side, sort, first, 3 * P)
             if first:
                 gather(TOKEN, WORDS, first, P)
                 gather(TOKEN, WORDS, first + P, 2 * P)
@@ -189,25 +192,19 @@ def tile_moe_duo_gelu_kernel(
             nc.scalar.activation(out=h_view, in_=pre_view, func=GELU)
             hidden[s0] = h
 
-        def turn(s0):
-            ((first, target),) = [(f, tile) for (f, w), tile in zip(RUNS, h_turned) if f <= s0 < f + w]
-            if s0 >= MOVING * C:
-                return
-            turned = banks.tile([P, 2, P], F32, name="turn%d" % (s0 // P % 2))
-            for u in range(2):
-                nc.tensor.transpose(turned[:, u, :], hidden[s0][:].bitcast(F32)[:, u * P : (u + 1) * P], ident[:])
-            move = nc.scalar.copy
-            move(out=target[:, s0 - first : s0 - first + P, :].bitcast(F32), in_=turned[:].rearrange("p u s -> p s u"))
+        def turn(e):
+            turned = banks.tile([P, 2, 2, P], F32, name="turn%d" % e)
+            for b in range(2):
+                words = hidden[e * C + b * P][:].bitcast(F32)
+                for u in range(2):
+                    nc.tensor.transpose(turned[:, b, u, :], words[:, u * P : (u + 1) * P], ident[:])
+            target = h_turned[0][:, e * C : (e + 1) * C, :].bitcast(F32).rearrange("p (b s) u -> p b s u", b=2)
+            nc.scalar.copy(out=target, in_=turned[:].rearrange("p b u s -> p b s u"))
 
-        waiting = []
-        for group in GROUPS:
-            for block in group:
-                first_layer(block * P)
-            waiting.extend(group)
-            for block in waiting[:-1]:
-                turn(block * P)
-            waiting = waiting[-1:]
-        turn(LAST)
+        for block in range(S // P):
+            first_layer(block * P)
+            if block in (2, 4):
+                turn(block // 2 - 1)
 
         y = [held(name, [P, S], F32) for name in ("y0", "h_turned%d" % LAST)]
 
@@ -258,21 +255,21 @@ def tile_moe_duo_gelu_kernel(
         def window(half, r, t0, t1):
             return y[half][:].indirect(places[r][:, t0 // 16 : t1 // 16])
 
-        gate_banks = []
-        for b, name in enumerate((PRE_BANKS[5], "last")):
+        gate_banks = {}
+        for b, name in ((1, PRE_BANKS[5]), (0, "last")):
             bank = banks.tile([P, 2, C], F32, name=name)
             for r in range(2):
                 for c in range(2):
                     column = gate_columns[r][:, 2 * b + c : 2 * b + c + 1]
                     nc.tensor.transpose(bank[:, r, c * P : (c + 1) * P], column.to_broadcast([P, P]), ident[:])
-            gate_banks.append(bank)
+            gate_banks[b] = bank
 
         def finish(engine, half, t0, t1, first, second):
             total = held("sum%d_%d" % (half, t0), [P, t1 - t0], F32)
             engine.tensor_tensor(total[:], first, second, ADD)
             nc.sync.dma_start(out=out[P * half : P * (half + 1), t0:t1], in_=total[:])
 
-        ranges = ((0, 256), (256, 384), (384, 512))
+        ranges = ((256, 512), (0, 128), (128, 256))
         split = SPLIT
         share = 288
         picked, weighed = {}, {}

from contextlib import ExitStack

import concourse.mybir as mybir
from concourse.masks import make_identity

K, T, E, C, H, N = 512, 512, 4, 256, 512, 256
S = E * C
P = 128
FLOPS = 2 * S * (2 * K * H + H * N)

F32 = mybir.dt.float32
BF16 = mybir.dt.bfloat16
I32 = mybir.dt.int32
U32 = mybir.dt.uint32
U16 = mybir.dt.uint16
U8 = mybir.dt.uint8
FP8X4 = mybir.dt.float8_e4m3fn_x4
FP4X4 = mybir.dt.float4_e2m1fn_x4
GELU = mybir.ActivationFunctionType.Gelu_apprx_tanh
COPY = mybir.ActivationFunctionType.Copy
MULT = mybir.AluOpType.mult
ADD = mybir.AluOpType.add

PARTNER, TOKEN = 0, 1
WORDS, SCALES = 0, 1
MOVING = 2
PRE_BANKS = ("pre0", "pre1", "pre0", "pre1", "late0", "late1", "pre1", "turn1")
SPLIT = 352
LAST = S - P

GROUPS = ((0,), (1, 2), (3, 4), (5, 6), (7,))
RUNS = ((0, 512), (512, 256), (768, 128), (896, 128))


def load_scale_rows(queue, plane, rows, quadrants):
    for q in quadrants:
        queue.dma_start(out=plane[32 * q : 32 * q + 4].bitcast(I32), in_=rows[4 * q : 4 * q + 4])


def tile_moe_duo_gelu_kernel(
    tc, x_words, x_scales, w1_words, w1_scales, wp_words, wp_scales, w2_words, w2_scales, gate, offs, pos1, pos2, offs2, out
):
    nc = tc.nc
    with ExitStack() as ctx:
        keep = ctx.enter_context(tc.tile_pool(name="keep", bufs=1))
        ring = ctx.enter_context(tc.tile_pool(name="ring", bufs=4))
        banks = ctx.enter_context(tc.psum_pool(name="banks", bufs=1))

        def held(name, shape, dtype):
            return keep.tile(shape, dtype, name=name, align_bytes=64)

        offs_sb = held("offs_sb", [P, S // 16], U16)
        offs2_sb = held("offs2_sb", [P, S // 16], U16)
        pos1_sb = held("pos1_sb", [P, T // 16], U16)
        pos2_sb = held("pos2_sb", [P, T // 16], U16)
        xw = held("xw", [P, T], I32)
        xs = held("xs", [P, T], U8)
        first_scales = held("first_scales", [P, 2, E, H], U8)
        wps, w1s = first_scales[:, PARTNER], first_scales[:, TOKEN]
        w2s = held("w2s", [P, E, N], U8)
        w1w = held("w1w", [P, E, 2 * H], U8)
        wpw = held("wpw", [P, E, 2 * H], U8)
        w2w = held("w2w", [P, E, 2 * N], U8)
        gates = [held("gates%d" % r, [P, width], F32) for r, width in enumerate((T, SPLIT))]
        ident = held("ident", [P, P], F32)

        def by_expert(dram):
            return dram.bitcast(I32).rearrange("e o p n -> p (e o) n")

        for plane in (wps, w1s):
            nc.vector.memset(plane.bitcast(I32), 0)

        def load_words(queue, tile, dram, experts):
            queue.dma_start(out=tile[:, experts, :].bitcast(I32), in_=by_expert(dram)[:, experts, :])

        make_identity(nc, ident[:])
        nc.gpsimd.memset(w2s[:].bitcast(I32), 0)

        x_rows = x_scales.bitcast(I32).rearrange("o b t -> b (o t)")

        def load_token_scales(queue, q):
            rows = x_rows[4 * q : 4 * q + 4].unsqueeze(0).broadcast_to([8, 4, T // 4])
            queue.dma_start(out=xs[32 * q : 32 * q + 32].bitcast(I32), in_=rows)

        nc.sync.dma_start(offs2_sb[:], offs2)
        load_token_scales(nc.sync, 0)
        nc.sync.dma_start(offs_sb[:], offs)
        load_token_scales(nc.sync, 1)
        for q in (2, 3):
            load_token_scales(nc.scalar, q)
        load_scale_rows(nc.scalar, wps, by_expert(wp_scales), range(1))
        nc.scalar.dma_start(out=xw[:], in_=x_words.rearrange("o p t d -> p (o t d)").bitcast(I32))
        load_words(nc.sync, wpw, wp_words, slice(0, 1))
        load_scale_rows(nc.sync, wps, by_expert(wp_scales), range(1, 4))
        load_words(nc.sync, w1w, w1_words, slice(0, 1))
        load_scale_rows(nc.scalar, w1s, by_expert(w1_scales), range(4))
        for e in (2, 1, 3):
            load_words(nc.sync, wpw, wp_words, slice(e, e + 1))
            load_words(nc.sync, w1w, w1_words, slice(e, e + 1))
        load_scale_rows(nc.sync, w2s, by_expert(w2_scales), range(4))
        nc.sync.dma_start(out=w2w[:].bitcast(I32), in_=by_expert(w2_words))
        nc.sync.dma_start(pos1_sb[:], pos1)
        nc.sync.dma_start(pos2_sb[:], pos2)
        for r, width in enumerate((T, SPLIT)):
            nc.sync.dma_start(out=gates[r][:], in_=gate[r, :, :width])
        gate_columns = [held("gate_columns%d" % r, [P, T // P], F32) for r in range(2)]
        with nc.allow_non_contiguous_dma(reason="one gate value a partition"):
            for r in range(2):
                nc.sync.dma_start(out=gate_columns[r][:], in_=gate[r, 0, :].rearrange("(c t) -> t c", t=P))

        laid_words, laid_scales = {}, {}
        for e in range(MOVING, E):
            laid_scales[e] = held("laid_scales%d" % e, [P, 2, 4, P], U8)
            nc.gpsimd.tensor_copy(out=laid_scales[e][:], in_=first_scales[:, :, e, :].rearrange("p a (m t) -> p a t m", t=4))
            for side, ww in ((PARTNER, wpw), (TOKEN, w1w)):
                laid_words[e, side] = held("laid_words%d_%d" % (e, side), [P, 4, P], U16)
                nc.gpsimd.tensor_copy(
                    out=laid_words[e, side][:], in_=ww[:, e, :].bitcast(U16).rearrange("p (m t) -> p t m", t=4)
                )

        h_turned = [held("h_turned%d" % first, [P, width, 4], BF16) for first, width in RUNS]

        gathered = {}
        windows = (xw[:].bitcast(U32), xs[:])
        lists = (offs2_sb, offs_sb)

        def gather(side, sort, first, width):
            tile = held("g%d_%d_%d" % (side, sort, first), [P, width], (U32, U8)[sort])
            cols = slice(first // 16, (first + width) // 16)
            nc.vector.tensor_copy(out=tile[:], in_=windows[sort].indirect(lists[side][:, cols]))
            for c0 in range(0, width, P):
                gathered[side, sort, first + c0] = tile[:, c0 : c0 + P]

        def scales_then_words(first, early, late):
            for side in (PARTNER, TOKEN):
                gather(side, SCALES, first, early + late)
            for start, width in ((first, early), (first + early, late)):
                for side in (PARTNER, TOKEN):
                    gather(side, WORDS, start, width)

        for first in (0, 3 * P):
            for side, sort in (
                ((PARTNER, SCALES), (PARTNER, WORDS), (TOKEN, SCALES))
                if first
                else ((PARTNER, SCALES), (TOKEN, SCALES), (PARTNER, WORDS))
            ):
                gather(side, sort, first, 3 * P)
            if first:
                gather(TOKEN, WORDS, first, P)
                gather(TOKEN, WORDS, first + P, 2 * P)
            else:
                gather(TOKEN, WORDS, first, 3 * P)
        scales_then_words(6 * P, P, P)

        hidden = {}

        def first_layer(s0):
            e = s0 // C
            pre = banks.tile([P, H], F32, name=PRE_BANKS[s0 // P])
            if e >= MOVING:
                for side in (PARTNER, TOKEN):
                    for t in range(4):
                        nc.tensor.matmul_mx(
                            out=pre[:, t * P : (t + 1) * P],
                            lhsT=laid_words[e, side][:, t, :].bitcast(FP4X4),
                            lhsT_scale=laid_scales[e][:, side, t, :],
                            rhs=gathered[side, WORDS, s0].bitcast(FP8X4),
                            rhs_scale=gathered[side, SCALES, s0],
                            start=(side == PARTNER and t == 0),
                            stop=(side == TOKEN and t == 3),
                        )
                ((first, target),) = [(f, tile) for (f, w), tile in zip(RUNS, h_turned) if f <= s0 < f + w]
                nc.scalar.activation(
                    out=target[:, s0 - first : s0 - first + P, :],
                    in_=pre[:].rearrange("p (t s) -> p s t", t=4),
                    func=GELU,
                )
                return
            for side, (ww, ws) in ((PARTNER, (wpw, wps)), (TOKEN, (w1w, w1s))):
                nc.tensor.matmul_mx(
                    out=pre[:],
                    lhsT=gathered[side, WORDS, s0].bitcast(FP8X4),
                    lhsT_scale=gathered[side, SCALES, s0],
                    rhs=ww[:, e, :].bitcast(FP4X4),
                    rhs_scale=ws[:, e, :],
                    start=(side == PARTNER),
                    stop=(side == TOKEN),
                )
            h = ring.tile([P, H], BF16, name="h", align_bytes=64)
            h_view = h[:].rearrange("s (u p d) -> s u p d", u=2, d=2)
            pre_view = pre[:].rearrange("s (p u d) -> s u p d", u=2, d=2)
            nc.scalar.activation(out=h_view, in_=pre_view, func=GELU)
            hidden[s0] = h

        def turn(e):
            turned = banks.tile([P, 2, 2, P], F32, name="turn%d" % e)
            for b in range(2):
                words = hidden[e * C + b * P][:].bitcast(F32)
                for u in range(2):
                    nc.tensor.transpose(turned[:, b, u, :], words[:, u * P : (u + 1) * P], ident[:])
            target = h_turned[0][:, e * C : (e + 1) * C, :].bitcast(F32).rearrange("p (b s) u -> p b s u", b=2)
            nc.scalar.copy(out=target, in_=turned[:].rearrange("p b u s -> p b s u"))

        for block in range(S // P):
            first_layer(block * P)
            if block in (2, 4):
                turn(block // 2 - 1)

        y = [held(name, [P, S], F32) for name in ("y0", "h_turned%d" % LAST)]

        quantised = []
        for r, (first, width) in enumerate(RUNS):
            codes = held("hc%d" % first, [P, width], U32)
            scales = held("hs%d" % first, [P, width], U8)
            nc.vector.quantize_mx(
                out=codes[:].bitcast(FP8X4), scales=scales[:], in_=h_turned[r][:].rearrange("p s d -> p (s d)")
            )
            quantised.append((codes, scales, first, width))

        def results(name, pieces, move):
            bank = banks.tile([P, sum(end - first for half, first, end in pieces)], F32, name=name)
            at = 0
            for half, first, end in pieces:
                for codes, scales, q0, width in quantised:
                    lo, hi = max(first, q0), min(end, q0 + width)
                    for c0 in range(lo, hi, P):
                        if c0 > lo and c0 % C:
                            continue
                        c1 = min(hi, (c0 // C + 1) * C)
                        nc.tensor.matmul_mx(
                            out=bank[:, at + c0 - first : at + c1 - first],
                            lhsT=w2w[:, c0 // C, 2 * P * half : 2 * P * (half + 1)].bitcast(FP4X4),
                            lhsT_scale=w2s[:, c0 // C, P * half : P * (half + 1)],
                            rhs=codes[:, c0 - q0 : c1 - q0].bitcast(FP8X4),
                            rhs_scale=scales[:, c0 - q0 : c1 - q0],
                            start=True,
                            stop=True,
                        )
                at = at + end - first
            at = 0
            for half, first, end in pieces:
                move(out=y[half][:, first:end], in_=bank[:, at : at + end - first])
                at = at + end - first

        results(PRE_BANKS[4], [(0, 0, 256)], nc.vector.tensor_copy)
        results(PRE_BANKS[5], [(0, 256, 768)], nc.scalar.copy)
        results(PRE_BANKS[6], [(0, 768, 896)], nc.scalar.copy)
        results("last", [(0, 896, 1024)], nc.scalar.copy)
        results("turn0", [(1, 0, 512)], nc.vector.tensor_copy)
        results("pre0", [(1, 512, 768)], nc.scalar.copy)
        results(PRE_BANKS[7], [(1, 768, 1024)], nc.scalar.copy)

        places = (pos1_sb, pos2_sb)

        def window(half, r, t0, t1):
            return y[half][:].indirect(places[r][:, t0 // 16 : t1 // 16])

        gate_banks = {}
        for b, name in ((1, PRE_BANKS[5]), (0, "last")):
            bank = banks.tile([P, 2, C], F32, name=name)
            for r in range(2):
                for c in range(2):
                    column = gate_columns[r][:, 2 * b + c : 2 * b + c + 1]
                    nc.tensor.transpose(bank[:, r, c * P : (c + 1) * P], column.to_broadcast([P, P]), ident[:])
            gate_banks[b] = bank

        def finish(engine, half, t0, t1, first, second):
            total = held("sum%d_%d" % (half, t0), [P, t1 - t0], F32)
            engine.tensor_tensor(total[:], first, second, ADD)
            nc.sync.dma_start(out=out[P * half : P * (half + 1), t0:t1], in_=total[:])

        ranges = ((256, 512), (0, 128), (128, 256))
        split = SPLIT
        share = 288
        picked, weighed = {}, {}

        def pick(t0, t1):
            picked[t0] = held("picked%d" % t0, [P, 2, t1 - t0], F32)
            for r in range(2):
                nc.scalar.activation(out=picked[t0][:, r, :], in_=window(1, r, t0, t1), func=COPY)

        rest = held("rest", [P, T - split], F32)
        nc.scalar.activation(out=rest[:], in_=window(0, 1, split, T), func=COPY)
        for piece in ranges:
            pick(*piece)

        first_part = held("first_part", [P, T], F32)
        nc.vector.tensor_tensor(first_part[:], window(0, 0, 0, T), gates[0][:], MULT)
        second_part = held("second_part", [P, T], F32)
        nc.vector.tensor_tensor(second_part[:, :split], window(0, 1, 0, split), gates[1][:], MULT)
        finish(nc.gpsimd, 0, 0, share, first_part[:, :share], second_part[:, :share])

        def weigh(t0, t1):
            weighed[t0] = held("weighed%d" % t0, [P, 2, t1 - t0], F32)
            bank = gate_banks[t0 // C]
            nc.vector.tensor_tensor(weighed[t0][:], picked[t0][:], bank[:, :, t0 % C : t0 % C + t1 - t0], MULT)

        def add(t0, t1):
            finish(nc.vector, 1, t0, t1, weighed[t0][:, 0, :], weighed[t0][:, 1, :])

        nc.vector.tensor_tensor(second_part[:, split:], rest[:], gate_banks[1][:, 1, split - C :], MULT)
        weigh(*ranges[0])
        weigh(*ranges[1])
        finish(nc.vector, 0, share, T, first_part[:, share:], second_part[:, share:])
        add(*ranges[0])
        weigh(*ranges[2])
        add(*ranges[1])
        add(*ranges[2])
